import numpy as np
import ml_dtypes


def mxq(x, axis, fmt="e4m3"):
    dtype, down = {"e4m3": (ml_dtypes.float8_e4m3fn, 7), "e5m2": (ml_dtypes.float8_e5m2, 14)}[fmt]
    v = np.moveaxis(np.asarray(x, np.float32).astype(ml_dtypes.bfloat16).astype(np.float64), axis, -1)
    blocks = v.reshape(v.shape[:-1] + (-1, 32))
    amax = np.abs(blocks).max(-1, keepdims=True)
    byte = np.maximum(np.where(amax > 0, np.frexp(amax)[1] - 1 + 127, 0) - down, 1)
    scale = np.exp2(byte - 127.0)
    codes = (blocks / scale).astype(np.float32).astype(dtype).astype(np.float64)
    return np.moveaxis((codes * scale).reshape(v.shape), -1, axis)


WIDE = False


def mx_kscale(k):
    if not WIDE:
        return np.ones(k)
    levels = np.array([10, -10, 5, -5, 0])
    if k % 512:
        return np.exp2(np.random.permutation(np.resize(levels, k // 32))).repeat(32)
    a = np.empty((k // 512, 16))
    for p in range(k // 512):
        a[p, :8] = np.random.permutation(np.resize(levels, 8))
        for g in range(8):
            far = levels[np.abs(levels - a[p, g]) >= 10]
            a[p, g + 8] = far[np.random.randint(len(far))]
    return np.exp2(a.ravel()).repeat(32)


def f64(x):
    return np.asarray(x).astype(np.float64)


def striped(idx):
    return np.tile(idx.reshape(-1, 16).T, (8, 1)).astype(np.uint16)


def unstriped(offs):
    return offs[:16].T.reshape(-1).astype(np.int64)


E2M1 = np.array([0.0, 0.5, 1.0, 1.5, 2.0, 3.0, 4.0, 6.0, -0.0, -0.5, -1.0, -1.5, -2.0, -3.0, -4.0, -6.0])


def pack_weight(w, fmt):
    k, n = w.shape
    w = f64(np.asarray(w, np.float32).astype(ml_dtypes.bfloat16)).reshape(k // 32, 32, n)
    amax = np.abs(w).max(1)
    if fmt == "e4m3":
        byte = np.frexp(amax)[1] - 1 + 127 - 7
    else:
        mant, ex = np.frexp(amax / 6.0)
        byte = np.where(mant > 0.5, ex, ex - 1) + 127
    byte = np.clip(np.where(amax > 0, byte, 1), 1, 254)
    scaled = (w * np.exp2(127.0 - byte)[:, None, :]).reshape(k, n).astype(np.float32)
    by_word = np.ascontiguousarray(scaled.reshape(k // 512, 128, 4, n).transpose(0, 1, 3, 2))
    if fmt == "e4m3":
        words = by_word.astype(ml_dtypes.float8_e4m3fn).view(np.uint8)
    else:
        c = by_word.astype(ml_dtypes.float4_e2m1fn).view(np.uint8) & 0xF
        words = (c[..., 0::2] | (c[..., 1::2] << 4)).reshape(k // 512, 128, 2 * n)
    return np.ascontiguousarray(words), np.ascontiguousarray(byte.astype(np.uint8).reshape(k // 512, 16, n))


def unpack_weight(words, scales, fmt):
    g, _, n = scales.shape
    words = np.ascontiguousarray(words).reshape(g, 128, n, -1)
    if fmt == "e4m3":
        vals = words.view(ml_dtypes.float8_e4m3fn).astype(np.float64)
    else:
        nib = np.empty((g, 128, n, 4), np.uint8)
        nib[..., 0::2] = words & 0xF
        nib[..., 1::2] = words >> 4
        vals = E2M1[nib]
    vals = vals * np.repeat(np.exp2(scales.astype(np.float64) - 127.0), 8, axis=1)[..., None]
    return vals.transpose(0, 1, 3, 2).reshape(g * 512, n)


def gelu(v):
    return 0.5 * v * (1.0 + np.tanh(np.sqrt(2.0 / np.pi) * (v + 0.044715 * v**3)))


T, S, P, K, H, R, N = 4096, 1024, 512, 1536, 1024, 512, 512

def setup_inputs():
    n = np.random.standard_normal
    s = mx_kscale(K)[:, None]
    u = mx_kscale(H)[:, None]
    u2 = mx_kscale(R)[:, None]
    tab_words, tab_scales = pack_weight(n((K, T)) * s, "e4m3")
    w1 = (0.75 * n((K, H)) / np.sqrt(K) / s).astype(np.float32)
    w2_words, w2_scales = pack_weight(0.6 * n((H, R)) / np.sqrt(H) / u, "e2m1")
    w3 = (n((R, N)) / np.sqrt(R) / u2).astype(np.float32)
    w4_words, w4_scales = pack_weight(0.3 * n((H, N)) / np.sqrt(H) / u, "e4m3")
    temp = np.random.uniform(0.4, 1.6, H).astype(np.float32)
    shift = (0.5 * n(H)).astype(np.float32)
    steep = np.random.uniform(1, 3, H).astype(np.float32)
    share = np.random.uniform(0.1, 0.5, H).astype(np.float32)
    gain = np.random.uniform(3.0, 5.5, H).astype(np.float32)
    stance = (np.sign(n(H)) * np.random.uniform(0.5, 1.0, H) * u[:, 0]).astype(np.float32)
    lift = (np.random.uniform(0.6, 1.8, R) * u2[:, 0]).astype(np.float32)
    return dict(tab_words=tab_words, tab_scales=tab_scales,
                offs=striped(np.random.permutation(T)[:S]),
                pos1=striped(np.random.permutation(S)[:P]),
                pos2=striped(np.random.permutation(S)[:P]),
                w1=w1, w2_words=w2_words, w2_scales=w2_scales, w3=w3,
                w4_words=w4_words, w4_scales=w4_scales, temp=temp, shift=shift,
                steep=steep, share=share, gain=gain, stance=stance, lift=lift)

def reference(tab_words, tab_scales, offs, pos1, pos2, w1, w2_words, w2_scales, w3,
              w4_words, w4_scales, temp, shift, steep, share, gain, stance, lift):
    v = unpack_weight(tab_words, tab_scales, "e4m3")[:, unstriped(offs)]
    w2 = unpack_weight(w2_words, w2_scales, "e2m1")
    w4 = unpack_weight(w4_words, w4_scales, "e4m3")
    h = mxq(f64(w1), 0, "e4m3").T @ v
    a = np.exp(f64(temp)[:, None] * h[:, unstriped(pos1)] + f64(shift)[:, None])
    top = h.max(axis=1)
    c = 1.0 / (1.0 + np.exp(-f64(steep)[:, None] * (h[:, unstriped(pos2)] - f64(share)[:, None] * top[:, None])))
    pair = mxq((a + f64(gain)[:, None] * c) * f64(stance)[:, None], 0, "e4m3")
    pupil = np.tanh(w2.T @ pair) * f64(lift)[:, None]
    return mxq(f64(w3), 0, "e4m3").T @ mxq(pupil, 0, "e4m3") + w4.T @ pair

@@ -1,0 +1,342 @@
+from contextlib import ExitStack
+
+import concourse.mybir as mybir
+
+T, S, PAIRS, K, H, R, N = 4096, 1024, 512, 1536, 1024, 512, 512
+FLOPS = 2 * (K * H * S + H * R * PAIRS + R * N * PAIRS + H * N * PAIRS)
+
+F32 = mybir.dt.float32
+BF16 = mybir.dt.bfloat16
+I32 = mybir.dt.int32
+U32 = mybir.dt.uint32
+U16 = mybir.dt.uint16
+U8 = mybir.dt.uint8
+FP8X4 = mybir.dt.float8_e4m3fn_x4
+FP4X4 = mybir.dt.float4_e2m1fn_x4
+ACT = mybir.ActivationFunctionType
+ALU = mybir.AluOpType
+
+P = 128
+PACK = 4
+PASS = P * PACK
+K_PASSES = K // PASS
+H_PASSES = H // PASS
+BANK = 512
+QUARTER = 128
+HALF = 256
+
+
+def tile_list_bidding_tutor_reading_kernel(
+    tc, tab_words, tab_scales, offs, pos1, pos2, w1, w2_words, w2_scales, w3,
+    w4_words, w4_scales, temp, shift, steep, share, gain, stance, lift, out,
+):
+    nc = tc.nc
+    with ExitStack() as ctx:
+        keep = ctx.enter_context(tc.tile_pool(name="keep", bufs=1))
+        ring = ctx.enter_context(tc.tile_pool(name="ring", bufs=4))
+        psum = ctx.enter_context(tc.psum_pool(name="psum", bufs=1))
+
+        def kept(shape, dtype, name):
+            return keep.tile(shape, dtype, name=name, align_bytes=64)
+
+        def bank_tile(bank, name):
+            return psum.tile([P, BANK], F32, name=name, tag="bank%d" % bank)
+
+        def load_list(src, name):
+            tile = keep.tile(list(src.shape), U16, name=name)
+            nc.sync.dma_start(tile[:], src)
+            return tile
+
+        def load_row_factor(src, name):
+            tile = kept([P, src.shape[0] // PASS, PACK], F32, name)
+            nc.sync.dma_start(out=tile[:], in_=src.rearrange("(b p i) -> p b i", p=P, i=PACK))
+            return tile
+
+        def load_rows(rows, name):
+            raw = ring.tile([P, PACK, PASS], F32, name=name, tag="f32_stage", align_bytes=64)
+            nc.sync.dma_start(out=raw[:], in_=rows.rearrange("(p j) c -> p j c", j=PACK))
+            return raw
+
+        def load_w1(a, b):
+            return load_rows(w1[a * PASS:(a + 1) * PASS, b * PASS:(b + 1) * PASS], "w1_raw%d%d" % (a, b))
+
+        def load_table(a):
+            tile = kept([P, T], U32, "tab%d" % a)
+            nc.sync.dma_start(out=tile[:].bitcast(I32), in_=tab_words[a].rearrange("p t i -> p (t i)").bitcast(I32))
+            return tile
+
+        tab_plane = kept([P, T], U8, "tab_plane")
+        w2_plane_raw = kept([P, H_PASSES, R], U8, "w2_plane_raw")
+        w4_plane = kept([P, H_PASSES, N], U8, "w4_plane")
+        nc.vector.memset(tab_plane[:].bitcast(I32), 0)
+        nc.vector.memset(w2_plane_raw[:].bitcast(I32), 0)
+        nc.vector.memset(w4_plane[:].bitcast(I32), 0)
+        for plane, src in ((w2_plane_raw, w2_scales), (w4_plane, w4_scales)):
+            for q in range(4):
+                nc.gpsimd.dma_start(
+                    out=plane[32 * q:32 * q + 4, :, :].bitcast(I32),
+                    in_=src[:, 4 * q:4 * q + 4, :].rearrange("a r n -> r a n").bitcast(I32),
+                )
+
+        w1_raw = {}
+        tab = {}
+        w2_raw = kept([P, H_PASSES, 2 * R], U8, "w2_raw")
+        nc.sync.dma_start(out=w2_raw[:].bitcast(I32), in_=w2_words.rearrange("a p n -> p a n").bitcast(I32))
+        w1_raw[0, 0] = load_w1(0, 0)
+        offs_t = load_list(offs, "offs_t")
+        tab[0] = load_table(0)
+        for q in range(4):
+            nc.sync.dma_start(
+                out=tab_plane[32 * q:32 * q + 4 * K_PASSES, :].bitcast(I32),
+                in_=tab_scales[:, 4 * q:4 * q + 4, :].bitcast(I32),
+            )
+        w1_raw[1, 0] = load_w1(1, 0)
+        tab[1] = load_table(1)
+        tab[2] = load_table(2)
+        pos1_t = load_list(pos1, "pos1_t")
+        temp_t = load_row_factor(temp, "temp_t")
+        shift_t = load_row_factor(shift, "shift_t")
+        w1_raw[2, 0] = load_w1(2, 0)
+        pos2_t = load_list(pos2, "pos2_t")
+        steep_t = load_row_factor(steep, "steep_t")
+        share_t = load_row_factor(share, "share_t")
+        for a in range(K_PASSES):
+            w1_raw[a, 1] = load_w1(a, 1)
+        gain_t = load_row_factor(gain, "gain_t")
+        stance_t = load_row_factor(stance, "stance_t")
+        w4_codes = kept([P, H_PASSES, N], U32, "w4_codes")
+        nc.sync.dma_start(out=w4_codes[:].bitcast(I32), in_=w4_words.rearrange("a p c i -> p a (c i)").bitcast(I32))
+        w3_raw = load_rows(w3, "w3_raw")
+        lift_t = load_row_factor(lift, "lift_t")
+
+        w2_codes = kept([P, H_PASSES, 2 * R], U8, "w2_codes")
+        w2_plane = kept([P, H_PASSES, R], U8, "w2_plane")
+        nc.vector.tensor_copy(
+            out=w2_codes[:].rearrange("p a (i q e) -> p a q i e", i=PACK, e=2),
+            in_=w2_raw[:].rearrange("p a (q i e) -> p a q i e", i=PACK, e=2),
+        )
+        nc.gpsimd.tensor_copy(
+            out=w2_plane[:].rearrange("p a (i q) -> p a q i", i=PACK),
+            in_=w2_plane_raw[:].rearrange("p a (q i) -> p a q i", i=PACK),
+        )
+
+        picked_plane = kept([P, S], U8, "picked_plane")
+        picked = {}
+
+        def gather_words(a):
+            picked[a] = kept([P, S], U32, "picked%d" % a)
+            nc.vector.tensor_copy(out=picked[a][:], in_=tab[a][:].indirect(offs_t[:]))
+
+        w1_codes = {}
+        w1_plane = {}
+
+        def quantise_w1(a, b, shares):
+            w1_codes[a, b] = kept([P, PASS], U32, "w1_codes%d%d" % (a, b))
+            w1_plane[a, b] = kept([P, PASS], U8, "w1_plane%d%d" % (a, b))
+            src = w1_raw[a, b][:].rearrange("p j (m i) -> p m j i", i=PACK)
+            rounded = []
+            for engine, i0, i1 in shares:
+                tile = ring.tile([P, i1 - i0, P, PACK], BF16, name="w1_bf16", tag="bf16_stage", align_bytes=64)
+                dst = tile[:].rearrange("p i m j -> p m j i")
+                if engine == "scalar":
+                    nc.scalar.activation(out=dst, in_=src[:, :, :, i0:i1], func=ACT.Copy)
+                else:
+                    nc.vector.tensor_copy(out=dst, in_=src[:, :, :, i0:i1])
+                rounded.append(tile)
+            for (engine, i0, i1), tile in zip(shares, rounded):
+                cols = slice(i0 * P, i1 * P)
+                nc.vector.quantize_mx(
+                    out=w1_codes[a, b][:, cols].bitcast(FP8X4),
+                    scales=w1_plane[a, b][:, cols],
+                    in_=tile[:].rearrange("p i m j -> p (i m j)"),
+                )
+
+        gather_words(0)
+        nc.vector.tensor_copy(out=picked_plane[:], in_=tab_plane[:].indirect(offs_t[:]))
+        quantise_w1(0, 0, [("scalar", 0, 4)])
+        quantise_w1(1, 0, [("scalar", 0, 4)])
+        gather_words(1)
+        gather_words(2)
+        quantise_w1(2, 0, [("vector", 0, 2), ("scalar", 2, 4)])
+
+        h = {}
+        half_top = kept([P, H_PASSES, PACK, 2], F32, "half_top")
+        gate_bias = kept([P, H_PASSES, PACK], F32, "gate_bias")
+        gate_slope = kept([P, H_PASSES, PACK], F32, "gate_slope")
+        gate_gain = kept([P, H_PASSES, PACK], F32, "gate_gain")
+
+        def scores(b, i):
+            h[b, i] = kept([P, S], F32, "h%d%d" % (b, i))
+            cols = slice(i * P, (i + 1) * P)
+            for u in range(S // BANK):
+                acc = bank_tile(2 * i + u, "h_acc")
+                hands = slice(u * BANK, (u + 1) * BANK)
+                for a in range(K_PASSES):
+                    nc.tensor.matmul_mx(
+                        out=acc[:],
+                        lhsT=w1_codes[a, b][:, cols].bitcast(FP8X4),
+                        lhsT_scale=w1_plane[a, b][:, cols],
+                        rhs=picked[a][:, hands].bitcast(FP8X4),
+                        rhs_scale=picked_plane[4 * a:P, hands],
+                        start=(a == 0),
+                        stop=(a == K_PASSES - 1),
+                    )
+                nc.vector.tensor_scalar(
+                    out=h[b, i][:, hands], in0=acc[:], scalar1=1.0, scalar2=None,
+                    op0=ALU.mult, op1=ALU.max, accum_out=half_top[:, b, i, u:u + 1],
+                )
+
+        def look_exp(dst, b, i, places):
+            nc.scalar.activation(
+                out=dst[:, i, places],
+                in_=h[b, i][:].indirect(pos1_t[:, places.start // 16:places.stop // 16]),
+                func=ACT.Exp, scale=temp_t[:, b, i:i + 1], bias=shift_t[:, b, i:i + 1],
+            )
+
+        def look_sigmoid(dst, b, i):
+            nc.scalar.activation(
+                out=dst[:, i, :], in_=h[b, i][:].indirect(pos2_t[:]),
+                func=ACT.Sigmoid, scale=steep_t[:, b, i:i + 1], bias=gate_bias[:, b, i:i + 1],
+            )
+
+        all_places = slice(0, PAIRS)
+        open0 = kept([P, PACK, PAIRS], F32, "open0")
+        for i in range(PACK):
+            scores(0, i)
+            look_exp(open0, 0, i, all_places)
+
+        nc.vector.scalar_tensor_tensor(
+            out=gate_slope[:], in0=steep_t[:], scalar=-1.0, in1=share_t[:], op0=ALU.mult, op1=ALU.mult)
+        top0 = kept([P, PACK], F32, "top0")
+        nc.vector.tensor_tensor(out=top0[:], in0=half_top[:, 0, :, 0], in1=half_top[:, 0, :, 1], op=ALU.max)
+        nc.vector.tensor_tensor(out=gate_bias[:, 0, :], in0=top0[:], in1=gate_slope[:, 0, :], op=ALU.mult)
+        gate0 = kept([P, PACK, PAIRS], F32, "gate0")
+        for i in range(PACK):
+            look_sigmoid(gate0, 0, i)
+
+        for a in range(K_PASSES):
+            quantise_w1(a, 1, [("vector", 0, 4)])
+        gate1 = keep.tile([P, PACK, PAIRS], F32, name="gate1", tag="looks1", align_bytes=64)
+        for i in range(PACK):
+            scores(1, i)
+            nc.vector.scalar_tensor_tensor(
+                out=gate_bias[:, 1, i:i + 1], in0=half_top[:, 1, i, 0:1], scalar=half_top[:, 1, i, 1:2],
+                in1=gate_slope[:, 1, i:i + 1], op0=ALU.max, op1=ALU.mult)
+            look_sigmoid(gate1, 1, i)
+
+        nc.vector.tensor_tensor(out=gate_gain[:], in0=gain_t[:], in1=stance_t[:], op=ALU.mult)
+        for i in range(PACK):
+            nc.vector.tensor_scalar(
+                out=open0[:, i, :], in0=open0[:, i, :], scalar1=stance_t[:, 0, i:i + 1], scalar2=None, op0=ALU.mult)
+        gate1_scaled = kept([P, PACK, PAIRS], F32, "gate1_scaled")
+        for i in range(PACK):
+            nc.vector.tensor_scalar(
+                out=gate1_scaled[:, i, :], in0=gate1[:, i, :], scalar1=gate_gain[:, 1, i:i + 1], scalar2=None,
+                op0=ALU.mult)
+        open1 = keep.tile([P, PACK, PAIRS], F32, name="open1", tag="looks1", align_bytes=64)
+        halves = [slice(u * HALF, (u + 1) * HALF) for u in range(PAIRS // HALF)]
+        for places in halves:
+            for i in range(PACK):
+                look_exp(open1, 1, i, places)
+
+        pair_rows = [kept([P, PACK, PAIRS], BF16, "pair_rows%d" % b) for b in range(H_PASSES)]
+        pair_bf16 = [kept([P, PAIRS, PACK], BF16, "pair_bf16%d" % b) for b in range(H_PASSES)]
+        pair_codes = [kept([P, PAIRS], U32, "pair_codes%d" % b) for b in range(H_PASSES)]
+        pair_plane = [kept([P, PAIRS], U8, "pair_plane%d" % b) for b in range(H_PASSES)]
+
+        def join(b, last, factor, first_scaled, places):
+            for i in range(PACK):
+                nc.vector.scalar_tensor_tensor(
+                    out=pair_rows[b][:, i, places], in0=last[:, i, places], scalar=factor[:, b, i:i + 1],
+                    in1=first_scaled[:, i, places], op0=ALU.mult, op1=ALU.add)
+
+        def interleave(dst, src):
+            nc.vector.tensor_copy(
+                out=dst.rearrange("p (c x) i -> p c i x", x=4),
+                in_=src.rearrange("p i (c x) -> p c i x", x=4),
+            )
+
+        def quantise(codes, plane, rounded):
+            nc.vector.quantize_mx(out=codes.bitcast(FP8X4), scales=plane, in_=rounded.rearrange("p c i -> p (c i)"))
+
+        join(0, gate0, gate_gain, open0, all_places)
+        interleave(pair_bf16[0][:], pair_rows[0][:])
+        quantise(pair_codes[0][:], pair_plane[0][:], pair_bf16[0][:])
+
+        w3_bf16 = ring.tile([P, N, PACK], BF16, name="w3_bf16", tag="bf16_stage", align_bytes=64)
+        w3_codes = kept([P, N], U32, "w3_codes")
+        w3_plane = kept([P, N], U8, "w3_plane")
+        interleave(w3_bf16[:], w3_raw[:])
+        quantise(w3_codes[:], w3_plane[:], w3_bf16[:])
+
+        quarters = [slice(q * QUARTER, (q + 1) * QUARTER) for q in range(PAIRS // QUARTER)]
+        pupil_acc = [bank_tile(q, "pupil_acc") for q in range(len(quarters))]
+        out_acc = [bank_tile(len(quarters) + q, "out_acc") for q in range(len(quarters))]
+
+        def pupil_passes(q, b):
+            for t in range(PACK):
+                nc.tensor.matmul_mx(
+                    out=pupil_acc[q][:, t * QUARTER:(t + 1) * QUARTER],
+                    lhsT=w2_codes[:, b, 2 * t * P:2 * (t + 1) * P].bitcast(FP4X4),
+                    lhsT_scale=w2_plane[:, b, t * P:(t + 1) * P],
+                    rhs=pair_codes[b][:, quarters[q]].bitcast(FP8X4),
+                    rhs_scale=pair_plane[b][:, quarters[q]],
+                    start=(b == 0 and t == 0),
+                    stop=(b == H_PASSES - 1 and t == PACK - 1),
+                )
+
+        def out_passes(q, w_codes, w_plane, x_codes, x_plane, first, last):
+            for t in range(N // P):
+                nc.tensor.matmul_mx(
+                    out=out_acc[q][:, t * QUARTER:(t + 1) * QUARTER],
+                    lhsT=w_codes[:, t * P:(t + 1) * P].bitcast(FP8X4),
+                    lhsT_scale=w_plane[:, t * P:(t + 1) * P],
+                    rhs=x_codes.bitcast(FP8X4),
+                    rhs_scale=x_plane,
+                    start=(first and t == 0),
+                    stop=(last and t == N // P - 1),
+                )
+
+        def w4_passes(q, b):
+            out_passes(q, w4_codes[:, b, :], w4_plane[:, b, :], pair_codes[b][:, quarters[q]],
+                       pair_plane[b][:, quarters[q]], b == 0, False)
+
+        for q in range(len(quarters)):
+            pupil_passes(q, 0)
+        for q in range(len(quarters)):
+            w4_passes(q, 0)
+
+        bent = ring.tile([P, PAIRS, PACK], F32, name="bent", tag="f32_stage", align_bytes=64)
+        result = ring.tile([P, len(quarters), N // P, QUARTER], F32, name="result", tag="f32_stage", align_bytes=64)
+        pupil_bf16 = kept([P, PAIRS, PACK], BF16, "pupil_bf16")
+        pupil_codes = kept([P, PAIRS], U32, "pupil_codes")
+        pupil_plane = kept([P, PAIRS], U8, "pupil_plane")
+        out_rows = out.rearrange("(t p) j -> p t j", p=P)
+
+        def finish_pair(q):
+            cols = quarters[q]
+            interleave(pair_bf16[1][:, cols, :], pair_rows[1][:, :, cols])
+            quantise(pair_codes[1][:, cols], pair_plane[1][:, cols], pair_bf16[1][:, cols, :])
+            pupil_passes(q, 1)
+            w4_passes(q, 1)
+            nc.scalar.activation(
+                out=bent[:, cols, :], in_=pupil_acc[q][:].rearrange("p (t j) -> p j t", t=PACK), func=ACT.Tanh)
+
+        def finish_pupil(q):
+            cols = quarters[q]
+            nc.vector.tensor_tensor(
+                out=pupil_bf16[:, cols, :], in0=bent[:, cols, :],
+                in1=lift_t[:].to_broadcast([P, QUARTER, PACK]), op=ALU.mult)
+            quantise(pupil_codes[:, cols], pupil_plane[:, cols], pupil_bf16[:, cols, :])
+            out_passes(q, w3_codes[:], w3_plane[:], pupil_codes[:, cols], pupil_plane[:, cols], False, True)
+            nc.scalar.copy(out=result[:, q, :, :].rearrange("p t j -> p (t j)"), in_=out_acc[q][:])
+            nc.sync.dma_start(out=out_rows[:, :, cols], in_=result[:, q, :, :])
+
+        join(1, open1, stance_t, gate1_scaled, halves[0])
+        finish_pair(0)
+        finish_pair(1)
+        join(1, open1, stance_t, gate1_scaled, halves[1])
+        finish_pair(2)
+        finish_pair(3)
+        for q in range(len(quarters)):
+            finish_pupil(q)

@@ -68,15 +68,23 @@ def tile_list_bidding_tutor_reading_kernel(
         tab_plane = kept([P, T], U8, "tab_plane")
         w2_plane_raw = kept([P, H_PASSES, R], U8, "w2_plane_raw")
         w4_plane = kept([P, H_PASSES, N], U8, "w4_plane")
-        nc.vector.memset(tab_plane[:].bitcast(I32), 0)
         nc.vector.memset(w2_plane_raw[:].bitcast(I32), 0)
+        nc.vector.memset(tab_plane[:].bitcast(I32), 0)
         nc.vector.memset(w4_plane[:].bitcast(I32), 0)
-        for plane, src in ((w2_plane_raw, w2_scales), (w4_plane, w4_scales)):
+        for q in range(4):
+            nc.gpsimd.dma_start(
+                out=tab_plane[32 * q:32 * q + 4 * K_PASSES, :].bitcast(I32),
+                in_=tab_scales[:, 4 * q:4 * q + 4, :].bitcast(I32),
+            )
+
+        def load_plane(engine, plane, src):
             for q in range(4):
-                nc.gpsimd.dma_start(
+                engine.dma_start(
                     out=plane[32 * q:32 * q + 4, :, :].bitcast(I32),
                     in_=src[:, 4 * q:4 * q + 4, :].rearrange("a r n -> r a n").bitcast(I32),
                 )
+
+        load_plane(nc.sync, w2_plane_raw, w2_scales)
 
         w1_raw = {}
         tab = {}
@@ -85,29 +93,26 @@ def tile_list_bidding_tutor_reading_kernel(
         w1_raw[0, 0] = load_w1(0, 0)
         offs_t = load_list(offs, "offs_t")
         tab[0] = load_table(0)
-        for q in range(4):
-            nc.sync.dma_start(
-                out=tab_plane[32 * q:32 * q + 4 * K_PASSES, :].bitcast(I32),
-                in_=tab_scales[:, 4 * q:4 * q + 4, :].bitcast(I32),
-            )
         w1_raw[1, 0] = load_w1(1, 0)
         tab[1] = load_table(1)
         tab[2] = load_table(2)
+        w1_raw[2, 0] = load_w1(2, 0)
         pos1_t = load_list(pos1, "pos1_t")
         temp_t = load_row_factor(temp, "temp_t")
         shift_t = load_row_factor(shift, "shift_t")
-        w1_raw[2, 0] = load_w1(2, 0)
+        w1_raw[0, 1] = load_w1(0, 1)
         pos2_t = load_list(pos2, "pos2_t")
         steep_t = load_row_factor(steep, "steep_t")
         share_t = load_row_factor(share, "share_t")
-        for a in range(K_PASSES):
-            w1_raw[a, 1] = load_w1(a, 1)
+        w1_raw[1, 1] = load_w1(1, 1)
+        w1_raw[2, 1] = load_w1(2, 1)
         gain_t = load_row_factor(gain, "gain_t")
         stance_t = load_row_factor(stance, "stance_t")
         w4_codes = kept([P, H_PASSES, N], U32, "w4_codes")
         nc.sync.dma_start(out=w4_codes[:].bitcast(I32), in_=w4_words.rearrange("a p c i -> p a (c i)").bitcast(I32))
         w3_raw = load_rows(w3, "w3_raw")
         lift_t = load_row_factor(lift, "lift_t")
+        load_plane(nc.sync, w4_plane, w4_scales)
 
         w2_codes = kept([P, H_PASSES, 2 * R], U8, "w2_codes")
         w2_plane = kept([P, H_PASSES, R], U8, "w2_plane")
@@ -115,7 +120,7 @@ def tile_list_bidding_tutor_reading_kernel(
             out=w2_codes[:].rearrange("p a (i q e) -> p a q i e", i=PACK, e=2),
             in_=w2_raw[:].rearrange("p a (q i e) -> p a q i e", i=PACK, e=2),
         )
-        nc.gpsimd.tensor_copy(
+        nc.vector.tensor_copy(
             out=w2_plane[:].rearrange("p a (i q) -> p a q i", i=PACK),
             in_=w2_plane_raw[:].rearrange("p a (q i) -> p a q i", i=PACK),
         )
@@ -165,24 +170,36 @@ def tile_list_bidding_tutor_reading_kernel(
         gate_slope = kept([P, H_PASSES, PACK], F32, "gate_slope")
         gate_gain = kept([P, H_PASSES, PACK], F32, "gate_gain")
 
+        h_acc = {}
+
+        def score_pass(b, i, u, a):
+            cols = slice(i * P, (i + 1) * P)
+            hands = slice(u * BANK, (u + 1) * BANK)
+            nc.tensor.matmul_mx(
+                out=h_acc[b, i, u][:],
+                lhsT=w1_codes[a, b][:, cols].bitcast(FP8X4),
+                lhsT_scale=w1_plane[a, b][:, cols],
+                rhs=picked[a][:, hands].bitcast(FP8X4),
+                rhs_scale=picked_plane[4 * a:P, hands],
+                start=(a == 0),
+                stop=(a == K_PASSES - 1),
+            )
+
+        def early_scores(b):
+            for i in range(PACK):
+                for u in range(S // BANK):
+                    h_acc[b, i, u] = bank_tile(2 * i + u, "h_acc")
+            for a in range(K_PASSES - 1):
+                for i in range(PACK):
+                    for u in range(S // BANK):
+                        score_pass(b, i, u, a)
+
         def scores(b, i):
             h[b, i] = kept([P, S], F32, "h%d%d" % (b, i))
-            cols = slice(i * P, (i + 1) * P)
             for u in range(S // BANK):
-                acc = bank_tile(2 * i + u, "h_acc")
-                hands = slice(u * BANK, (u + 1) * BANK)
-                for a in range(K_PASSES):
-                    nc.tensor.matmul_mx(
-                        out=acc[:],
-                        lhsT=w1_codes[a, b][:, cols].bitcast(FP8X4),
-                        lhsT_scale=w1_plane[a, b][:, cols],
-                        rhs=picked[a][:, hands].bitcast(FP8X4),
-                        rhs_scale=picked_plane[4 * a:P, hands],
-                        start=(a == 0),
-                        stop=(a == K_PASSES - 1),
-                    )
+                score_pass(b, i, u, K_PASSES - 1)
                 nc.vector.tensor_scalar(
-                    out=h[b, i][:, hands], in0=acc[:], scalar1=1.0, scalar2=None,
+                    out=h[b, i][:, u * BANK:(u + 1) * BANK], in0=h_acc[b, i, u][:], scalar1=1.0, scalar2=None,
                     op0=ALU.mult, op1=ALU.max, accum_out=half_top[:, b, i, u:u + 1],
                 )
 
@@ -201,6 +218,7 @@ def tile_list_bidding_tutor_reading_kernel(
 
         all_places = slice(0, PAIRS)
         open0 = kept([P, PACK, PAIRS], F32, "open0")
+        early_scores(0)
         for i in range(PACK):
             scores(0, i)
             look_exp(open0, 0, i, all_places)
@@ -216,6 +234,7 @@ def tile_list_bidding_tutor_reading_kernel(
 
         for a in range(K_PASSES):
             quantise_w1(a, 1, [("vector", 0, 4)])
+        early_scores(1)
         gate1 = keep.tile([P, PACK, PAIRS], F32, name="gate1", tag="looks1", align_bytes=64)
         for i in range(PACK):
             scores(1, i)

@@ -33,11 +33,10 @@ def tile_list_bidding_tutor_reading_kernel(
     nc = tc.nc
     with ExitStack() as ctx:
         keep = ctx.enter_context(tc.tile_pool(name="keep", bufs=1))
-        ring = ctx.enter_context(tc.tile_pool(name="ring", bufs=4))
         psum = ctx.enter_context(tc.psum_pool(name="psum", bufs=1))
 
-        def kept(shape, dtype, name):
-            return keep.tile(shape, dtype, name=name, align_bytes=64)
+        def kept(shape, dtype, name, tag=None):
+            return keep.tile(shape, dtype, name=name, tag=tag or name, align_bytes=64)
 
         def bank_tile(bank, name):
             return psum.tile([P, BANK], F32, name=name, tag="bank%d" % bank)
@@ -52,13 +51,13 @@ def tile_list_bidding_tutor_reading_kernel(
             nc.sync.dma_start(out=tile[:], in_=src.rearrange("(b p i) -> p b i", p=P, i=PACK))
             return tile
 
-        def load_rows(rows, name):
-            raw = ring.tile([P, PACK, PASS], F32, name=name, tag="f32_stage", align_bytes=64)
+        def load_rows(rows, name, tag):
+            raw = kept([P, PACK, PASS], F32, name, tag)
             nc.sync.dma_start(out=raw[:], in_=rows.rearrange("(p j) c -> p j c", j=PACK))
             return raw
 
-        def load_w1(a, b):
-            return load_rows(w1[a * PASS:(a + 1) * PASS, b * PASS:(b + 1) * PASS], "w1_raw%d%d" % (a, b))
+        def load_w1(a, b, tag):
+            return load_rows(w1[a * PASS:(a + 1) * PASS, b * PASS:(b + 1) * PASS], "w1_raw%d%d" % (a, b), tag)
 
         def load_table(a):
             tile = kept([P, T], U32, "tab%d" % a)
@@ -90,27 +89,27 @@ def tile_list_bidding_tutor_reading_kernel(
         tab = {}
         w2_raw = kept([P, H_PASSES, 2 * R], U8, "w2_raw")
         nc.sync.dma_start(out=w2_raw[:].bitcast(I32), in_=w2_words.rearrange("a p n -> p a n").bitcast(I32))
-        w1_raw[0, 0] = load_w1(0, 0)
+        w1_raw[0, 0] = load_w1(0, 0, "stage_a")
         offs_t = load_list(offs, "offs_t")
         tab[0] = load_table(0)
-        w1_raw[1, 0] = load_w1(1, 0)
+        w1_raw[1, 0] = load_w1(1, 0, "stage_b")
         tab[1] = load_table(1)
         tab[2] = load_table(2)
-        w1_raw[2, 0] = load_w1(2, 0)
+        w1_raw[2, 0] = load_w1(2, 0, "stage_c")
         pos1_t = load_list(pos1, "pos1_t")
         temp_t = load_row_factor(temp, "temp_t")
         shift_t = load_row_factor(shift, "shift_t")
-        w1_raw[0, 1] = load_w1(0, 1)
+        w1_raw[0, 1] = load_w1(0, 1, "stage_d")
         pos2_t = load_list(pos2, "pos2_t")
         steep_t = load_row_factor(steep, "steep_t")
         share_t = load_row_factor(share, "share_t")
-        w1_raw[1, 1] = load_w1(1, 1)
-        w1_raw[2, 1] = load_w1(2, 1)
+        w1_raw[1, 1] = load_w1(1, 1, "stage_a")
+        w1_raw[2, 1] = load_w1(2, 1, "stage_b")
         gain_t = load_row_factor(gain, "gain_t")
         stance_t = load_row_factor(stance, "stance_t")
         w4_codes = kept([P, H_PASSES, N], U32, "w4_codes")
         nc.sync.dma_start(out=w4_codes[:].bitcast(I32), in_=w4_words.rearrange("a p c i -> p a (c i)").bitcast(I32))
-        w3_raw = load_rows(w3, "w3_raw")
+        w3_raw = load_rows(w3, "w3_raw", "stage_c")
         lift_t = load_row_factor(lift, "lift_t")
         load_plane(nc.sync, w4_plane, w4_scales)
 
@@ -140,15 +139,22 @@ def tile_list_bidding_tutor_reading_kernel(
             w1_plane[a, b] = kept([P, PASS], U8, "w1_plane%d%d" % (a, b))
             src = w1_raw[a, b][:].rearrange("p j (m i) -> p m j i", i=PACK)
             rounded = []
-            for engine, i0, i1 in shares:
-                tile = ring.tile([P, i1 - i0, P, PACK], BF16, name="w1_bf16", tag="bf16_stage", align_bytes=64)
+            for engine, i0, i1, tag in shares:
+                tile = kept([P, i1 - i0, P, PACK], BF16, "w1_bf16", tag)
                 dst = tile[:].rearrange("p i m j -> p m j i")
                 if engine == "scalar":
                     nc.scalar.activation(out=dst, in_=src[:, :, :, i0:i1], func=ACT.Copy)
+                elif engine == "gpsimd":
+                    step = 256 // (i1 - i0)
+                    for m0 in range(0, P, step):
+                        nc.gpsimd.tensor_scalar(
+                            out=dst[:, m0:m0 + step, :, :].rearrange("p m j i -> p m i j"),
+                            in0=src[:, m0:m0 + step, :, i0:i1].rearrange("p m j i -> p m i j"),
+                            scalar1=1.0, scalar2=0.0, op0=ALU.mult, op1=ALU.add)
                 else:
                     nc.vector.tensor_copy(out=dst, in_=src[:, :, :, i0:i1])
                 rounded.append(tile)
-            for (engine, i0, i1), tile in zip(shares, rounded):
+            for (engine, i0, i1, tag), tile in zip(shares, rounded):
                 cols = slice(i0 * P, i1 * P)
                 nc.vector.quantize_mx(
                     out=w1_codes[a, b][:, cols].bitcast(FP8X4),
@@ -158,11 +164,11 @@ def tile_list_bidding_tutor_reading_kernel(
 
         gather_words(0)
         nc.vector.tensor_copy(out=picked_plane[:], in_=tab_plane[:].indirect(offs_t[:]))
-        quantise_w1(0, 0, [("scalar", 0, 4)])
-        quantise_w1(1, 0, [("scalar", 0, 4)])
+        quantise_w1(0, 0, [("scalar", 0, 4, "round_a")])
+        quantise_w1(1, 0, [("scalar", 0, 4, "round_b")])
         gather_words(1)
         gather_words(2)
-        quantise_w1(2, 0, [("vector", 0, 2), ("scalar", 2, 4)])
+        quantise_w1(2, 0, [("vector", 0, 2, "round_c"), ("scalar", 2, 4, "round_d")])
 
         h = {}
         half_top = kept([P, H_PASSES, PACK, 2], F32, "half_top")
@@ -232,8 +238,9 @@ def tile_list_bidding_tutor_reading_kernel(
         for i in range(PACK):
             look_sigmoid(gate0, 0, i)
 
-        for a in range(K_PASSES):
-            quantise_w1(a, 1, [("vector", 0, 4)])
+        quantise_w1(0, 1, [("gpsimd", 0, 4, "round_a")])
+        quantise_w1(1, 1, [("vector", 0, 2, "round_c"), ("gpsimd", 2, 4, "round_d")])
+        quantise_w1(2, 1, [("vector", 0, 4, "round_b")])
         early_scores(1)
         gate1 = keep.tile([P, PACK, PAIRS], F32, name="gate1", tag="looks1", align_bytes=64)
         for i in range(PACK):
@@ -244,9 +251,11 @@ def tile_list_bidding_tutor_reading_kernel(
             look_sigmoid(gate1, 1, i)
 
         nc.vector.tensor_tensor(out=gate_gain[:], in0=gain_t[:], in1=stance_t[:], op=ALU.mult)
+        open0_scaled = kept([P, PACK, PAIRS], F32, "open0_scaled", "stage_b")
         for i in range(PACK):
-            nc.vector.tensor_scalar(
-                out=open0[:, i, :], in0=open0[:, i, :], scalar1=stance_t[:, 0, i:i + 1], scalar2=None, op0=ALU.mult)
+            nc.gpsimd.tensor_scalar(
+                out=open0_scaled[:, i, :], in0=open0[:, i, :], scalar1=stance_t[:, 0, i:i + 1], scalar2=0.0,
+                op0=ALU.mult, op1=ALU.add)
         gate1_scaled = kept([P, PACK, PAIRS], F32, "gate1_scaled")
         for i in range(PACK):
             nc.vector.tensor_scalar(
@@ -278,14 +287,17 @@ def tile_list_bidding_tutor_reading_kernel(
         def quantise(codes, plane, rounded):
             nc.vector.quantize_mx(out=codes.bitcast(FP8X4), scales=plane, in_=rounded.rearrange("p c i -> p (c i)"))
 
-        join(0, gate0, gate_gain, open0, all_places)
+        join(0, gate0, gate_gain, open0_scaled, all_places)
         interleave(pair_bf16[0][:], pair_rows[0][:])
         quantise(pair_codes[0][:], pair_plane[0][:], pair_bf16[0][:])
 
-        w3_bf16 = ring.tile([P, N, PACK], BF16, name="w3_bf16", tag="bf16_stage", align_bytes=64)
+        w3_bf16 = kept([P, N, PACK], BF16, "w3_bf16", "round_b")
         w3_codes = kept([P, N], U32, "w3_codes")
         w3_plane = kept([P, N], U8, "w3_plane")
-        interleave(w3_bf16[:], w3_raw[:])
+        for c0 in range(0, N, N // 2):
+            nc.gpsimd.tensor_scalar(
+                out=w3_bf16[:, c0:c0 + N // 2, :], in0=w3_raw[:, :, c0:c0 + N // 2].rearrange("p i c -> p c i"),
+                scalar1=1.0, scalar2=0.0, op0=ALU.mult, op1=ALU.add)
         quantise(w3_codes[:], w3_plane[:], w3_bf16[:])
 
         quarters = [slice(q * QUARTER, (q + 1) * QUARTER) for q in range(PAIRS // QUARTER)]
@@ -325,37 +337,50 @@ def tile_list_bidding_tutor_reading_kernel(
         for q in range(len(quarters)):
             w4_passes(q, 0)
 
-        bent = ring.tile([P, PAIRS, PACK], F32, name="bent", tag="f32_stage", align_bytes=64)
-        result = ring.tile([P, len(quarters), N // P, QUARTER], F32, name="result", tag="f32_stage", align_bytes=64)
+        bent = kept([P, PAIRS, PACK], F32, "bent", "stage_a")
+        result = kept([P, len(quarters), N // P, QUARTER], F32, "result", "stage_d")
         pupil_bf16 = kept([P, PAIRS, PACK], BF16, "pupil_bf16")
         pupil_codes = kept([P, PAIRS], U32, "pupil_codes")
         pupil_plane = kept([P, PAIRS], U8, "pupil_plane")
         out_rows = out.rearrange("(t p) j -> p t j", p=P)
 
-        def finish_pair(q):
-            cols = quarters[q]
+        def round_pair(cols):
             interleave(pair_bf16[1][:, cols, :], pair_rows[1][:, :, cols])
+
+        def multiply_pair(q):
+            cols = quarters[q]
             quantise(pair_codes[1][:, cols], pair_plane[1][:, cols], pair_bf16[1][:, cols, :])
             pupil_passes(q, 1)
             w4_passes(q, 1)
             nc.scalar.activation(
                 out=bent[:, cols, :], in_=pupil_acc[q][:].rearrange("p (t j) -> p j t", t=PACK), func=ACT.Tanh)
 
-        def finish_pupil(q):
-            cols = quarters[q]
+        def round_pupil(cols):
             nc.vector.tensor_tensor(
                 out=pupil_bf16[:, cols, :], in0=bent[:, cols, :],
-                in1=lift_t[:].to_broadcast([P, QUARTER, PACK]), op=ALU.mult)
+                in1=lift_t[:].to_broadcast([P, cols.stop - cols.start, PACK]), op=ALU.mult)
+
+        def quantise_pupil(cols):
             quantise(pupil_codes[:, cols], pupil_plane[:, cols], pupil_bf16[:, cols, :])
+
+        def finish(q):
+            cols = quarters[q]
             out_passes(q, w3_codes[:], w3_plane[:], pupil_codes[:, cols], pupil_plane[:, cols], False, True)
             nc.scalar.copy(out=result[:, q, :, :].rearrange("p t j -> p (t j)"), in_=out_acc[q][:])
             nc.sync.dma_start(out=out_rows[:, :, cols], in_=result[:, q, :, :])
 
-        join(1, open1, stance_t, gate1_scaled, halves[0])
-        finish_pair(0)
-        finish_pair(1)
-        join(1, open1, stance_t, gate1_scaled, halves[1])
-        finish_pair(2)
-        finish_pair(3)
-        for q in range(len(quarters)):
-            finish_pupil(q)
+        for u, places in enumerate(halves):
+            join(1, open1, stance_t, gate1_scaled, places)
+            round_pair(quarters[2 * u])
+            round_pair(quarters[2 * u + 1])
+            multiply_pair(2 * u)
+            multiply_pair(2 * u + 1)
+        round_pupil(halves[0])
+        quantise_pupil(halves[0])
+        finish(0)
+        finish(1)
+        round_pupil(quarters[2])
+        round_pupil(quarters[3])
+        for q in (2, 3):
+            quantise_pupil(quarters[q])
+            finish(q)

@@ -83,12 +83,9 @@ def tile_list_bidding_tutor_reading_kernel(
                     in_=src[:, 4 * q:4 * q + 4, :].rearrange("a r n -> r a n").bitcast(I32),
                 )
 
-        load_plane(nc.sync, w2_plane_raw, w2_scales)
 
         w1_raw = {}
         tab = {}
-        w2_raw = kept([P, H_PASSES, 2 * R], U8, "w2_raw")
-        nc.sync.dma_start(out=w2_raw[:].bitcast(I32), in_=w2_words.rearrange("a p n -> p a n").bitcast(I32))
         w1_raw[0, 0] = load_w1(0, 0, "stage_a")
         offs_t = load_list(offs, "offs_t")
         tab[0] = load_table(0)
@@ -103,27 +100,29 @@ def tile_list_bidding_tutor_reading_kernel(
         pos2_t = load_list(pos2, "pos2_t")
         steep_t = load_row_factor(steep, "steep_t")
         share_t = load_row_factor(share, "share_t")
+        w2_raw = kept([P, H_PASSES, 2 * R], U8, "w2_raw")
+        nc.sync.dma_start(out=w2_raw[:].bitcast(I32), in_=w2_words.rearrange("a p n -> p a n").bitcast(I32))
+        load_plane(nc.sync, w2_plane_raw, w2_scales)
         w1_raw[1, 1] = load_w1(1, 1, "stage_a")
         w1_raw[2, 1] = load_w1(2, 1, "stage_b")
         gain_t = load_row_factor(gain, "gain_t")
         stance_t = load_row_factor(stance, "stance_t")
         w4_codes = kept([P, H_PASSES, N], U32, "w4_codes")
         nc.sync.dma_start(out=w4_codes[:].bitcast(I32), in_=w4_words.rearrange("a p c i -> p a (c i)").bitcast(I32))
-        w3_raw = load_rows(w3, "w3_raw", "stage_c")
-        lift_t = load_row_factor(lift, "lift_t")
+        w3_raw = kept([P, PACK, N], F32, "w3_raw", "stage_c")
+        for t in range(PACK):
+            nc.sync.dma_start(out=w3_raw[:, t, :], in_=w3.rearrange("(g t u) n -> t g u n", t=PACK, u=8)[t])
+        lift_t = kept([P, 1, PACK], F32, "lift_t")
+        lift_raw = kept([P, PACK, 8], F32, "lift_raw")
+        with nc.allow_non_contiguous_dma(reason="one factor a partition"):
+            for t in range(PACK):
+                nc.sync.dma_start(
+                    out=lift_raw[:, t, 0:1], in_=lift.rearrange("(g t u o) -> t g u o", t=PACK, u=8, o=1)[t])
+        nc.gpsimd.tensor_copy(out=lift_t[:, 0, :], in_=lift_raw[:, :, 0])
         load_plane(nc.sync, w4_plane, w4_scales)
 
         w2_codes = kept([P, H_PASSES, 2 * R], U8, "w2_codes")
         w2_plane = kept([P, H_PASSES, R], U8, "w2_plane")
-        nc.vector.tensor_copy(
-            out=w2_codes[:].rearrange("p a (i q e) -> p a q i e", i=PACK, e=2),
-            in_=w2_raw[:].rearrange("p a (q i e) -> p a q i e", i=PACK, e=2),
-        )
-        nc.vector.tensor_copy(
-            out=w2_plane[:].rearrange("p a (i q) -> p a q i", i=PACK),
-            in_=w2_plane_raw[:].rearrange("p a (q i) -> p a q i", i=PACK),
-        )
-
         picked_plane = kept([P, S], U8, "picked_plane")
         picked = {}
 
@@ -145,7 +144,7 @@ def tile_list_bidding_tutor_reading_kernel(
                 if engine == "scalar":
                     nc.scalar.activation(out=dst, in_=src[:, :, :, i0:i1], func=ACT.Copy)
                 elif engine == "gpsimd":
-                    step = 256 // (i1 - i0)
+                    step = 128 // (i1 - i0)
                     for m0 in range(0, P, step):
                         nc.gpsimd.tensor_scalar(
                             out=dst[:, m0:m0 + step, :, :].rearrange("p m j i -> p m i j"),
@@ -229,8 +228,10 @@ def tile_list_bidding_tutor_reading_kernel(
             scores(0, i)
             look_exp(open0, 0, i, all_places)
 
-        nc.vector.scalar_tensor_tensor(
-            out=gate_slope[:], in0=steep_t[:], scalar=-1.0, in1=share_t[:], op0=ALU.mult, op1=ALU.mult)
+        minus_share = kept([P, H_PASSES, PACK], F32, "minus_share")
+        nc.gpsimd.tensor_scalar(
+            out=minus_share[:], in0=share_t[:], scalar1=-1.0, scalar2=0.0, op0=ALU.mult, op1=ALU.add)
+        nc.gpsimd.tensor_tensor(out=gate_slope[:], in0=steep_t[:], in1=minus_share[:], op=ALU.mult)
         top0 = kept([P, PACK], F32, "top0")
         nc.vector.tensor_tensor(out=top0[:], in0=half_top[:, 0, :, 0], in1=half_top[:, 0, :, 1], op=ALU.max)
         nc.vector.tensor_tensor(out=gate_bias[:, 0, :], in0=top0[:], in1=gate_slope[:, 0, :], op=ALU.mult)
@@ -238,19 +239,19 @@ def tile_list_bidding_tutor_reading_kernel(
         for i in range(PACK):
             look_sigmoid(gate0, 0, i)
 
-        quantise_w1(0, 1, [("gpsimd", 0, 4, "round_a")])
-        quantise_w1(1, 1, [("vector", 0, 2, "round_c"), ("gpsimd", 2, 4, "round_d")])
+        quantise_w1(0, 1, [("vector", 0, 2, "round_c"), ("gpsimd", 2, 4, "round_d")])
+        quantise_w1(1, 1, [("vector", 0, 4, "round_a")])
         quantise_w1(2, 1, [("vector", 0, 4, "round_b")])
         early_scores(1)
         gate1 = keep.tile([P, PACK, PAIRS], F32, name="gate1", tag="looks1", align_bytes=64)
         for i in range(PACK):
             scores(1, i)
-            nc.vector.scalar_tensor_tensor(
-                out=gate_bias[:, 1, i:i + 1], in0=half_top[:, 1, i, 0:1], scalar=half_top[:, 1, i, 1:2],
-                in1=gate_slope[:, 1, i:i + 1], op0=ALU.max, op1=ALU.mult)
+            nc.vector.tensor_scalar(
+                out=gate_bias[:, 1, i:i + 1], in0=half_top[:, 1, i, 0:1], scalar1=half_top[:, 1, i, 1:2],
+                scalar2=gate_slope[:, 1, i:i + 1], op0=ALU.max, op1=ALU.mult)
             look_sigmoid(gate1, 1, i)
 
-        nc.vector.tensor_tensor(out=gate_gain[:], in0=gain_t[:], in1=stance_t[:], op=ALU.mult)
+        nc.gpsimd.tensor_tensor(out=gate_gain[:], in0=gain_t[:], in1=stance_t[:], op=ALU.mult)
         open0_scaled = kept([P, PACK, PAIRS], F32, "open0_scaled", "stage_b")
         for i in range(PACK):
             nc.gpsimd.tensor_scalar(
@@ -291,6 +292,11 @@ def tile_list_bidding_tutor_reading_kernel(
         interleave(pair_bf16[0][:], pair_rows[0][:])
         quantise(pair_codes[0][:], pair_plane[0][:], pair_bf16[0][:])
 
+        for dst, src in ((w2_codes, w2_raw), (w2_plane, w2_plane_raw)):
+            nc.gpsimd.tensor_copy(
+                out=dst[:].bitcast(I32).rearrange("p a (t g w) -> p a t g w", t=PACK, g=16),
+                in_=src[:].bitcast(I32).rearrange("p a (g t w) -> p a t g w", t=PACK, g=16),
+            )
         w3_bf16 = kept([P, N, PACK], BF16, "w3_bf16", "round_b")
         w3_codes = kept([P, N], U32, "w3_codes")
         w3_plane = kept([P, N], U8, "w3_plane")
@@ -366,7 +372,8 @@ def tile_list_bidding_tutor_reading_kernel(
         def finish(q):
             cols = quarters[q]
             out_passes(q, w3_codes[:], w3_plane[:], pupil_codes[:, cols], pupil_plane[:, cols], False, True)
-            nc.scalar.copy(out=result[:, q, :, :].rearrange("p t j -> p (t j)"), in_=out_acc[q][:])
+            copy = nc.vector.tensor_copy if q == len(quarters) - 1 else nc.scalar.copy
+            copy(out=result[:, q, :, :].rearrange("p t j -> p (t j)"), in_=out_acc[q][:])
             nc.sync.dma_start(out=out_rows[:, :, cols], in_=result[:, q, :, :])
 
         for u, places in enumerate(halves):

@@ -21,9 +21,12 @@ PACK = 4
 PASS = P * PACK
 K_PASSES = K // PASS
 H_PASSES = H // PASS
+QUADRANTS = 4
+BLOCK_ROWS = 8
 BANK = 512
-QUARTER = 128
-HALF = 256
+QUARTER = BANK // PACK
+HALF = PAIRS // 2
+LIST_ROWS = 16
 
 
 def tile_list_bidding_tutor_reading_kernel(
@@ -47,42 +50,38 @@ def tile_list_bidding_tutor_reading_kernel(
             return tile
 
         def load_row_factor(src, name):
-            tile = kept([P, src.shape[0] // PASS, PACK], F32, name)
+            tile = kept([P, H_PASSES, PACK], F32, name)
             nc.sync.dma_start(out=tile[:], in_=src.rearrange("(b p i) -> p b i", p=P, i=PACK))
             return tile
 
-        def load_rows(rows, name, tag):
-            raw = kept([P, PACK, PASS], F32, name, tag)
-            nc.sync.dma_start(out=raw[:], in_=rows.rearrange("(p j) c -> p j c", j=PACK))
-            return raw
-
         def load_w1(a, b, tag):
-            return load_rows(w1[a * PASS:(a + 1) * PASS, b * PASS:(b + 1) * PASS], "w1_raw%d%d" % (a, b), tag)
+            raw = kept([P, PACK, PASS], F32, "w1_raw%d%d" % (a, b), tag)
+            piece = w1[a * PASS:(a + 1) * PASS, b * PASS:(b + 1) * PASS]
+            nc.sync.dma_start(out=raw[:], in_=piece.rearrange("(p j) c -> p j c", j=PACK))
+            return raw
 
         def load_table(a):
             tile = kept([P, T], U32, "tab%d" % a)
             nc.sync.dma_start(out=tile[:].bitcast(I32), in_=tab_words[a].rearrange("p t i -> p (t i)").bitcast(I32))
             return tile
 
-        tab_plane = kept([P, T], U8, "tab_plane")
-        w2_plane_raw = kept([P, H_PASSES, R], U8, "w2_plane_raw")
-        w4_plane = kept([P, H_PASSES, N], U8, "w4_plane")
-        nc.vector.memset(w2_plane_raw[:].bitcast(I32), 0)
-        nc.vector.memset(tab_plane[:].bitcast(I32), 0)
-        nc.vector.memset(w4_plane[:].bitcast(I32), 0)
-        for q in range(4):
-            nc.gpsimd.dma_start(
-                out=tab_plane[32 * q:32 * q + 4 * K_PASSES, :].bitcast(I32),
-                in_=tab_scales[:, 4 * q:4 * q + 4, :].bitcast(I32),
-            )
-
-        def load_plane(engine, plane, src):
-            for q in range(4):
-                engine.dma_start(
+        def load_plane(plane, src):
+            for q in range(QUADRANTS):
+                nc.sync.dma_start(
                     out=plane[32 * q:32 * q + 4, :, :].bitcast(I32),
                     in_=src[:, 4 * q:4 * q + 4, :].rearrange("a r n -> r a n").bitcast(I32),
                 )
 
+        tab_plane = kept([P, T], U8, "tab_plane")
+        w2_plane_raw = kept([P, H_PASSES, R], U8, "w2_plane_raw")
+        w4_plane = kept([P, H_PASSES, N], U8, "w4_plane")
+        for plane in (tab_plane, w2_plane_raw, w4_plane):
+            nc.vector.memset(plane[:].bitcast(I32), 0)
+        for q in range(QUADRANTS):
+            nc.gpsimd.dma_start(
+                out=tab_plane[32 * q:32 * q + 4 * K_PASSES, :].bitcast(I32),
+                in_=tab_scales[:, 4 * q:4 * q + 4, :].bitcast(I32),
+            )
 
         w1_raw = {}
         tab = {}
@@ -97,85 +96,89 @@ def tile_list_bidding_tutor_reading_kernel(
         temp_t = load_row_factor(temp, "temp_t")
         shift_t = load_row_factor(shift, "shift_t")
         w1_raw[0, 1] = load_w1(0, 1, "stage_d")
+        w1_raw[1, 1] = load_w1(1, 1, "stage_a")
         pos2_t = load_list(pos2, "pos2_t")
         steep_t = load_row_factor(steep, "steep_t")
         share_t = load_row_factor(share, "share_t")
         w2_raw = kept([P, H_PASSES, 2 * R], U8, "w2_raw")
         nc.sync.dma_start(out=w2_raw[:].bitcast(I32), in_=w2_words.rearrange("a p n -> p a n").bitcast(I32))
-        load_plane(nc.sync, w2_plane_raw, w2_scales)
-        w1_raw[1, 1] = load_w1(1, 1, "stage_a")
         w1_raw[2, 1] = load_w1(2, 1, "stage_b")
+        load_plane(w2_plane_raw, w2_scales)
         gain_t = load_row_factor(gain, "gain_t")
         stance_t = load_row_factor(stance, "stance_t")
         w4_codes = kept([P, H_PASSES, N], U32, "w4_codes")
         nc.sync.dma_start(out=w4_codes[:].bitcast(I32), in_=w4_words.rearrange("a p c i -> p a (c i)").bitcast(I32))
         w3_raw = kept([P, PACK, N], F32, "w3_raw", "stage_c")
         for t in range(PACK):
-            nc.sync.dma_start(out=w3_raw[:, t, :], in_=w3.rearrange("(g t u) n -> t g u n", t=PACK, u=8)[t])
-        lift_t = kept([P, 1, PACK], F32, "lift_t")
+            nc.sync.dma_start(
+                out=w3_raw[:, t, :], in_=w3.rearrange("(g t u) n -> t g u n", t=PACK, u=BLOCK_ROWS)[t])
         lift_raw = kept([P, PACK, 8], F32, "lift_raw")
+        lift_t = kept([P, 1, PACK], F32, "lift_t")
         with nc.allow_non_contiguous_dma(reason="one factor a partition"):
             for t in range(PACK):
                 nc.sync.dma_start(
-                    out=lift_raw[:, t, 0:1], in_=lift.rearrange("(g t u o) -> t g u o", t=PACK, u=8, o=1)[t])
+                    out=lift_raw[:, t, 0:1],
+                    in_=lift.rearrange("(g t u o) -> t g u o", t=PACK, u=BLOCK_ROWS, o=1)[t])
         nc.gpsimd.tensor_copy(out=lift_t[:, 0, :], in_=lift_raw[:, :, 0])
-        load_plane(nc.sync, w4_plane, w4_scales)
+        load_plane(w4_plane, w4_scales)
 
-        w2_codes = kept([P, H_PASSES, 2 * R], U8, "w2_codes")
-        w2_plane = kept([P, H_PASSES, R], U8, "w2_plane")
-        picked_plane = kept([P, S], U8, "picked_plane")
+        def quantise(codes, plane, rounded):
+            nc.vector.quantize_mx(out=codes.bitcast(FP8X4), scales=plane, in_=rounded.rearrange("p c i -> p (c i)"))
+
         picked = {}
+        picked_plane = kept([P, S], U8, "picked_plane")
+        w1_codes = {}
+        w1_plane = {}
+        for a in range(K_PASSES):
+            for b in range(H_PASSES):
+                w1_codes[a, b] = kept([P, PASS], U32, "w1_codes%d%d" % (a, b))
+                w1_plane[a, b] = kept([P, PASS], U8, "w1_plane%d%d" % (a, b))
 
         def gather_words(a):
             picked[a] = kept([P, S], U32, "picked%d" % a)
             nc.vector.tensor_copy(out=picked[a][:], in_=tab[a][:].indirect(offs_t[:]))
 
-        w1_codes = {}
-        w1_plane = {}
+        def round_w1(engine, a, b, tiles, tag):
+            rounded = kept([P, len(tiles), P, PACK], BF16, "w1_bf16", tag)
+            src = w1_raw[a, b][:].rearrange("p j (m i) -> p m i j", i=PACK)[:, :, tiles.start:tiles.stop, :]
+            dst = rounded[:].rearrange("p i m j -> p m i j")
+            if engine == "scalar":
+                nc.scalar.activation(
+                    out=dst.rearrange("p m i j -> p m j i"), in_=src.rearrange("p m i j -> p m j i"), func=ACT.Copy)
+            elif engine == "gpsimd":
+                for m0 in (0, P // 2):
+                    nc.gpsimd.tensor_scalar(
+                        out=dst[:, m0:m0 + P // 2, :, :], in0=src[:, m0:m0 + P // 2, :, :],
+                        scalar1=1.0, scalar2=0.0, op0=ALU.mult, op1=ALU.add)
+            else:
+                nc.vector.tensor_copy(out=dst, in_=src)
+            return {i: (rounded, i - tiles.start) for i in tiles}
 
-        def quantise_w1(a, b, shares):
-            w1_codes[a, b] = kept([P, PASS], U32, "w1_codes%d%d" % (a, b))
-            w1_plane[a, b] = kept([P, PASS], U8, "w1_plane%d%d" % (a, b))
-            src = w1_raw[a, b][:].rearrange("p j (m i) -> p m j i", i=PACK)
-            rounded = []
-            for engine, i0, i1, tag in shares:
-                tile = kept([P, i1 - i0, P, PACK], BF16, "w1_bf16", tag)
-                dst = tile[:].rearrange("p i m j -> p m j i")
-                if engine == "scalar":
-                    nc.scalar.activation(out=dst, in_=src[:, :, :, i0:i1], func=ACT.Copy)
-                elif engine == "gpsimd":
-                    step = 128 // (i1 - i0)
-                    for m0 in range(0, P, step):
-                        nc.gpsimd.tensor_scalar(
-                            out=dst[:, m0:m0 + step, :, :].rearrange("p m j i -> p m i j"),
-                            in0=src[:, m0:m0 + step, :, i0:i1].rearrange("p m j i -> p m i j"),
-                            scalar1=1.0, scalar2=0.0, op0=ALU.mult, op1=ALU.add)
-                else:
-                    nc.vector.tensor_copy(out=dst, in_=src[:, :, :, i0:i1])
-                rounded.append(tile)
-            for (engine, i0, i1, tag), tile in zip(shares, rounded):
-                cols = slice(i0 * P, i1 * P)
-                nc.vector.quantize_mx(
-                    out=w1_codes[a, b][:, cols].bitcast(FP8X4),
-                    scales=w1_plane[a, b][:, cols],
-                    in_=tile[:].rearrange("p i m j -> p (i m j)"),
-                )
+        def quantise_w1(a, b, rounded, tiles):
+            tile, place = rounded[tiles.start]
+            cols = slice(tiles.start * P, tiles.stop * P)
+            quantise(w1_codes[a, b][:, cols], w1_plane[a, b][:, cols],
+                     tile[:, place:place + len(tiles), :, :].rearrange("p i m j -> p (i m) j"))
 
+        every, front, back = range(PACK), range(PACK // 2), range(PACK // 2, PACK)
         gather_words(0)
         nc.vector.tensor_copy(out=picked_plane[:], in_=tab_plane[:].indirect(offs_t[:]))
-        quantise_w1(0, 0, [("scalar", 0, 4, "round_a")])
-        quantise_w1(1, 0, [("scalar", 0, 4, "round_b")])
+        quantise_w1(0, 0, round_w1("scalar", 0, 0, every, "round_a"), every)
+        quantise_w1(1, 0, round_w1("scalar", 1, 0, every, "round_b"), every)
         gather_words(1)
         gather_words(2)
-        quantise_w1(2, 0, [("vector", 0, 2, "round_c"), ("scalar", 2, 4, "round_d")])
+        last_front = round_w1("vector", 2, 0, front, "round_c")
+        last_back = round_w1("scalar", 2, 0, back, "round_d")
+        for i in front:
+            quantise_w1(2, 0, last_front, range(i, i + 1))
+        quantise_w1(2, 0, last_back, back)
 
         h = {}
-        half_top = kept([P, H_PASSES, PACK, 2], F32, "half_top")
+        h_acc = {}
+        bank_top = kept([P, H_PASSES, PACK, S // BANK], F32, "bank_top")
         gate_bias = kept([P, H_PASSES, PACK], F32, "gate_bias")
         gate_slope = kept([P, H_PASSES, PACK], F32, "gate_slope")
         gate_gain = kept([P, H_PASSES, PACK], F32, "gate_gain")
-
-        h_acc = {}
 
         def score_pass(b, i, u, a):
             cols = slice(i * P, (i + 1) * P)
@@ -190,119 +193,139 @@ def tile_list_bidding_tutor_reading_kernel(
                 stop=(a == K_PASSES - 1),
             )
 
-        def early_scores(b):
-            for i in range(PACK):
+        def early_passes(b):
+            for i in every:
                 for u in range(S // BANK):
                     h_acc[b, i, u] = bank_tile(2 * i + u, "h_acc")
             for a in range(K_PASSES - 1):
-                for i in range(PACK):
+                for i in every:
                     for u in range(S // BANK):
                         score_pass(b, i, u, a)
 
-        def scores(b, i):
+        scalar_bank = (0, 0, 1)
+
+        def finish_scores(b, i):
             h[b, i] = kept([P, S], F32, "h%d%d" % (b, i))
             for u in range(S // BANK):
                 score_pass(b, i, u, K_PASSES - 1)
-                nc.vector.tensor_scalar(
-                    out=h[b, i][:, u * BANK:(u + 1) * BANK], in0=h_acc[b, i, u][:], scalar1=1.0, scalar2=None,
-                    op0=ALU.mult, op1=ALU.max, accum_out=half_top[:, b, i, u:u + 1],
-                )
+                dst = h[b, i][:, u * BANK:(u + 1) * BANK]
+                if (b, i, u) == scalar_bank:
+                    nc.scalar.copy(out=dst, in_=h_acc[b, i, u][:])
+                else:
+                    nc.vector.tensor_scalar(
+                        out=dst, in0=h_acc[b, i, u][:], scalar1=1.0, scalar2=None,
+                        op0=ALU.mult, op1=ALU.max, accum_out=bank_top[:, b, i, u:u + 1])
 
         def look_exp(dst, b, i, places):
             nc.scalar.activation(
-                out=dst[:, i, places],
-                in_=h[b, i][:].indirect(pos1_t[:, places.start // 16:places.stop // 16]),
+                out=dst[:, places],
+                in_=h[b, i][:].indirect(pos1_t[:, places.start // LIST_ROWS:places.stop // LIST_ROWS]),
                 func=ACT.Exp, scale=temp_t[:, b, i:i + 1], bias=shift_t[:, b, i:i + 1],
             )
 
         def look_sigmoid(dst, b, i):
             nc.scalar.activation(
-                out=dst[:, i, :], in_=h[b, i][:].indirect(pos2_t[:]),
+                out=dst[:], in_=h[b, i][:].indirect(pos2_t[:]),
                 func=ACT.Sigmoid, scale=steep_t[:, b, i:i + 1], bias=gate_bias[:, b, i:i + 1],
             )
 
         all_places = slice(0, PAIRS)
-        open0 = kept([P, PACK, PAIRS], F32, "open0")
-        early_scores(0)
-        for i in range(PACK):
-            scores(0, i)
-            look_exp(open0, 0, i, all_places)
+        open0 = [kept([P, PAIRS], F32, "open0_%d" % i) for i in every]
+        early_passes(0)
+        next_front = round_w1("gpsimd", 0, 1, front, "round_c")
+        for i in every:
+            if i == PACK - 1:
+                quantise_w1(0, 1, next_front, front)
+            finish_scores(0, i)
+            look_exp(open0[i], 0, i, all_places)
 
         minus_share = kept([P, H_PASSES, PACK], F32, "minus_share")
         nc.gpsimd.tensor_scalar(
             out=minus_share[:], in0=share_t[:], scalar1=-1.0, scalar2=0.0, op0=ALU.mult, op1=ALU.add)
         nc.gpsimd.tensor_tensor(out=gate_slope[:], in0=steep_t[:], in1=minus_share[:], op=ALU.mult)
         top0 = kept([P, PACK], F32, "top0")
-        nc.vector.tensor_tensor(out=top0[:], in0=half_top[:, 0, :, 0], in1=half_top[:, 0, :, 1], op=ALU.max)
+        nc.vector.tensor_reduce(
+            out=bank_top[:, 0, 0, 1:2], in_=h[0, 0][:, BANK:S], axis=mybir.AxisListType.X, op=ALU.max)
+        nc.vector.tensor_tensor(out=top0[:], in0=bank_top[:, 0, :, 0], in1=bank_top[:, 0, :, 1], op=ALU.max)
         nc.vector.tensor_tensor(out=gate_bias[:, 0, :], in0=top0[:], in1=gate_slope[:, 0, :], op=ALU.mult)
-        gate0 = kept([P, PACK, PAIRS], F32, "gate0")
-        for i in range(PACK):
-            look_sigmoid(gate0, 0, i)
+        gate0 = [kept([P, PAIRS], F32, "gate0_%d" % i) for i in every]
+        for i in every:
+            look_sigmoid(gate0[i], 0, i)
 
-        quantise_w1(0, 1, [("vector", 0, 2, "round_c"), ("gpsimd", 2, 4, "round_d")])
-        quantise_w1(1, 1, [("vector", 0, 4, "round_a")])
-        quantise_w1(2, 1, [("vector", 0, 4, "round_b")])
-        early_scores(1)
-        gate1 = keep.tile([P, PACK, PAIRS], F32, name="gate1", tag="looks1", align_bytes=64)
-        for i in range(PACK):
-            scores(1, i)
+        quantise_w1(0, 1, round_w1("vector", 0, 1, back, "round_d"), back)
+        quantise_w1(1, 1, round_w1("vector", 1, 1, every, "round_a"), every)
+        last_piece = round_w1("vector", 2, 1, every, "round_b")
+        quantise_w1(2, 1, last_piece, front)
+        quantise_w1(2, 1, last_piece, back)
+        early_passes(1)
+
+        def second_half_looks(name):
+            first = kept([P, PACK - 1, PAIRS], F32, name + "_first", "looks1_first")
+            last = kept([P, PAIRS], F32, name + "_last", "looks1_last")
+            return [first[:, i, :] for i in range(PACK - 1)] + [last[:]]
+
+        gate1 = second_half_looks("gate1")
+        for i in every:
+            finish_scores(1, i)
             nc.vector.tensor_scalar(
-                out=gate_bias[:, 1, i:i + 1], in0=half_top[:, 1, i, 0:1], scalar1=half_top[:, 1, i, 1:2],
+                out=gate_bias[:, 1, i:i + 1], in0=bank_top[:, 1, i, 0:1], scalar1=bank_top[:, 1, i, 1:2],
                 scalar2=gate_slope[:, 1, i:i + 1], op0=ALU.max, op1=ALU.mult)
-            look_sigmoid(gate1, 1, i)
+            look_sigmoid(gate1[i], 1, i)
 
         nc.gpsimd.tensor_tensor(out=gate_gain[:], in0=gain_t[:], in1=stance_t[:], op=ALU.mult)
         open0_scaled = kept([P, PACK, PAIRS], F32, "open0_scaled", "stage_b")
-        for i in range(PACK):
+        for i in every:
             nc.gpsimd.tensor_scalar(
-                out=open0_scaled[:, i, :], in0=open0[:, i, :], scalar1=stance_t[:, 0, i:i + 1], scalar2=0.0,
+                out=open0_scaled[:, i, :], in0=open0[i][:], scalar1=stance_t[:, 0, i:i + 1], scalar2=0.0,
                 op0=ALU.mult, op1=ALU.add)
         gate1_scaled = kept([P, PACK, PAIRS], F32, "gate1_scaled")
-        for i in range(PACK):
+        for i in every:
             nc.vector.tensor_scalar(
-                out=gate1_scaled[:, i, :], in0=gate1[:, i, :], scalar1=gate_gain[:, 1, i:i + 1], scalar2=None,
+                out=gate1_scaled[:, i, :], in0=gate1[i], scalar1=gate_gain[:, 1, i:i + 1], scalar2=None,
                 op0=ALU.mult)
-        open1 = keep.tile([P, PACK, PAIRS], F32, name="open1", tag="looks1", align_bytes=64)
+        open1 = second_half_looks("open1")
         halves = [slice(u * HALF, (u + 1) * HALF) for u in range(PAIRS // HALF)]
         for places in halves:
-            for i in range(PACK):
-                look_exp(open1, 1, i, places)
+            for i in every:
+                look_exp(open1[i], 1, i, places)
 
         pair_rows = [kept([P, PACK, PAIRS], BF16, "pair_rows%d" % b) for b in range(H_PASSES)]
         pair_bf16 = [kept([P, PAIRS, PACK], BF16, "pair_bf16%d" % b) for b in range(H_PASSES)]
         pair_codes = [kept([P, PAIRS], U32, "pair_codes%d" % b) for b in range(H_PASSES)]
         pair_plane = [kept([P, PAIRS], U8, "pair_plane%d" % b) for b in range(H_PASSES)]
 
-        def join(b, last, factor, first_scaled, places):
-            for i in range(PACK):
+        def join(b, later, factor, earlier_scaled, places):
+            for i in every:
                 nc.vector.scalar_tensor_tensor(
-                    out=pair_rows[b][:, i, places], in0=last[:, i, places], scalar=factor[:, b, i:i + 1],
-                    in1=first_scaled[:, i, places], op0=ALU.mult, op1=ALU.add)
+                    out=pair_rows[b][:, i, places], in0=later[i][:, places], scalar=factor[:, b, i:i + 1],
+                    in1=earlier_scaled[:, i, places], op0=ALU.mult, op1=ALU.add)
 
-        def interleave(dst, src):
+        def interleave_pair(b, places):
             nc.vector.tensor_copy(
-                out=dst.rearrange("p (c x) i -> p c i x", x=4),
-                in_=src.rearrange("p i (c x) -> p c i x", x=4),
+                out=pair_bf16[b][:, places, :].rearrange("p (c x) i -> p c i x", x=4),
+                in_=pair_rows[b][:, :, places].rearrange("p i (c x) -> p c i x", x=4),
             )
 
-        def quantise(codes, plane, rounded):
-            nc.vector.quantize_mx(out=codes.bitcast(FP8X4), scales=plane, in_=rounded.rearrange("p c i -> p (c i)"))
+        def quantise_pair(b, places):
+            quantise(pair_codes[b][:, places], pair_plane[b][:, places], pair_bf16[b][:, places, :])
 
         join(0, gate0, gate_gain, open0_scaled, all_places)
-        interleave(pair_bf16[0][:], pair_rows[0][:])
-        quantise(pair_codes[0][:], pair_plane[0][:], pair_bf16[0][:])
+        interleave_pair(0, all_places)
+        quantise_pair(0, all_places)
 
+        w2_codes = kept([P, H_PASSES, 2 * R], U8, "w2_codes")
+        w2_plane = kept([P, H_PASSES, R], U8, "w2_plane")
         for dst, src in ((w2_codes, w2_raw), (w2_plane, w2_plane_raw)):
             nc.gpsimd.tensor_copy(
-                out=dst[:].bitcast(I32).rearrange("p a (t g w) -> p a t g w", t=PACK, g=16),
-                in_=src[:].bitcast(I32).rearrange("p a (g t w) -> p a t g w", t=PACK, g=16),
+                out=dst[:].bitcast(I32).rearrange("p a (t g w) -> p a t g w", t=PACK, g=P // BLOCK_ROWS),
+                in_=src[:].bitcast(I32).rearrange("p a (g t w) -> p a t g w", t=PACK, g=P // BLOCK_ROWS),
             )
         w3_bf16 = kept([P, N, PACK], BF16, "w3_bf16", "round_b")
         w3_codes = kept([P, N], U32, "w3_codes")
         w3_plane = kept([P, N], U8, "w3_plane")
-        for c0 in range(0, N, N // 2):
+        for c0 in (0, N // 2):
             nc.gpsimd.tensor_scalar(
-                out=w3_bf16[:, c0:c0 + N // 2, :], in0=w3_raw[:, :, c0:c0 + N // 2].rearrange("p i c -> p c i"),
+                out=w3_bf16[:, c0:c0 + N // 2, :], in0=w3_raw[:, :, c0:c0 + N // 2].rearrange("p t c -> p c t"),
                 scalar1=1.0, scalar2=0.0, op0=ALU.mult, op1=ALU.add)
         quantise(w3_codes[:], w3_plane[:], w3_bf16[:])
 
@@ -323,71 +346,60 @@ def tile_list_bidding_tutor_reading_kernel(
                 )
 
         def out_passes(q, w_codes, w_plane, x_codes, x_plane, first, last):
-            for t in range(N // P):
+            for s in range(N // P):
                 nc.tensor.matmul_mx(
-                    out=out_acc[q][:, t * QUARTER:(t + 1) * QUARTER],
-                    lhsT=w_codes[:, t * P:(t + 1) * P].bitcast(FP8X4),
-                    lhsT_scale=w_plane[:, t * P:(t + 1) * P],
-                    rhs=x_codes.bitcast(FP8X4),
-                    rhs_scale=x_plane,
-                    start=(first and t == 0),
-                    stop=(last and t == N // P - 1),
+                    out=out_acc[q][:, s * QUARTER:(s + 1) * QUARTER],
+                    lhsT=w_codes[:, s * P:(s + 1) * P].bitcast(FP8X4),
+                    lhsT_scale=w_plane[:, s * P:(s + 1) * P],
+                    rhs=x_codes[:, quarters[q]].bitcast(FP8X4),
+                    rhs_scale=x_plane[:, quarters[q]],
+                    start=(first and s == 0),
+                    stop=(last and s == N // P - 1),
                 )
-
-        def w4_passes(q, b):
-            out_passes(q, w4_codes[:, b, :], w4_plane[:, b, :], pair_codes[b][:, quarters[q]],
-                       pair_plane[b][:, quarters[q]], b == 0, False)
-
-        for q in range(len(quarters)):
-            pupil_passes(q, 0)
-        for q in range(len(quarters)):
-            w4_passes(q, 0)
 
         bent = kept([P, PAIRS, PACK], F32, "bent", "stage_a")
         result = kept([P, len(quarters), N // P, QUARTER], F32, "result", "stage_d")
         pupil_bf16 = kept([P, PAIRS, PACK], BF16, "pupil_bf16")
         pupil_codes = kept([P, PAIRS], U32, "pupil_codes")
         pupil_plane = kept([P, PAIRS], U8, "pupil_plane")
-        out_rows = out.rearrange("(t p) j -> p t j", p=P)
+        out_rows = out.rearrange("(s p) j -> p s j", p=P)
 
-        def round_pair(cols):
-            interleave(pair_bf16[1][:, cols, :], pair_rows[1][:, :, cols])
-
-        def multiply_pair(q):
-            cols = quarters[q]
-            quantise(pair_codes[1][:, cols], pair_plane[1][:, cols], pair_bf16[1][:, cols, :])
-            pupil_passes(q, 1)
-            w4_passes(q, 1)
+        def bend(q):
             nc.scalar.activation(
-                out=bent[:, cols, :], in_=pupil_acc[q][:].rearrange("p (t j) -> p j t", t=PACK), func=ACT.Tanh)
+                out=bent[:, quarters[q], :], in_=pupil_acc[q][:].rearrange("p (t j) -> p j t", t=PACK), func=ACT.Tanh)
 
-        def round_pupil(cols):
+        def round_pupil(places):
             nc.vector.tensor_tensor(
-                out=pupil_bf16[:, cols, :], in0=bent[:, cols, :],
-                in1=lift_t[:].to_broadcast([P, cols.stop - cols.start, PACK]), op=ALU.mult)
+                out=pupil_bf16[:, places, :], in0=bent[:, places, :],
+                in1=lift_t[:].to_broadcast([P, places.stop - places.start, PACK]), op=ALU.mult)
 
-        def quantise_pupil(cols):
-            quantise(pupil_codes[:, cols], pupil_plane[:, cols], pupil_bf16[:, cols, :])
+        def quantise_pupil(places):
+            quantise(pupil_codes[:, places], pupil_plane[:, places], pupil_bf16[:, places, :])
 
-        def finish(q):
-            cols = quarters[q]
-            out_passes(q, w3_codes[:], w3_plane[:], pupil_codes[:, cols], pupil_plane[:, cols], False, True)
-            copy = nc.vector.tensor_copy if q == len(quarters) - 1 else nc.scalar.copy
-            copy(out=result[:, q, :, :].rearrange("p t j -> p (t j)"), in_=out_acc[q][:])
-            nc.sync.dma_start(out=out_rows[:, :, cols], in_=result[:, q, :, :])
+        def finish_out(q, copy):
+            out_passes(q, w3_codes[:], w3_plane[:], pupil_codes, pupil_plane, False, True)
+            copy(out=result[:, q, :, :].rearrange("p s j -> p (s j)"), in_=out_acc[q][:])
+            nc.sync.dma_start(out=out_rows[:, :, quarters[q]], in_=result[:, q, :, :])
 
+        for q in range(len(quarters)):
+            pupil_passes(q, 0)
         for u, places in enumerate(halves):
             join(1, open1, stance_t, gate1_scaled, places)
-            round_pair(quarters[2 * u])
-            round_pair(quarters[2 * u + 1])
-            multiply_pair(2 * u)
-            multiply_pair(2 * u + 1)
+            for q in (2 * u, 2 * u + 1):
+                interleave_pair(1, quarters[q])
+            for q in (2 * u, 2 * u + 1):
+                quantise_pair(1, quarters[q])
+                pupil_passes(q, 1)
+                bend(q)
+        for q in range(len(quarters)):
+            for b in range(H_PASSES):
+                out_passes(q, w4_codes[:, b, :], w4_plane[:, b, :], pair_codes[b], pair_plane[b], b == 0, False)
         round_pupil(halves[0])
         quantise_pupil(halves[0])
-        finish(0)
-        finish(1)
+        finish_out(0, nc.scalar.copy)
+        finish_out(1, nc.scalar.copy)
         round_pupil(quarters[2])
         round_pupil(quarters[3])
-        for q in (2, 3):
+        for q, copy in ((2, nc.scalar.copy), (3, nc.vector.tensor_copy)):
             quantise_pupil(quarters[q])
-            finish(q)
+            finish_out(q, copy)

from contextlib import ExitStack

import concourse.mybir as mybir

T, S, PAIRS, K, H, R, N = 4096, 1024, 512, 1536, 1024, 512, 512
FLOPS = 2 * (K * H * S + H * R * PAIRS + R * N * PAIRS + H * N * PAIRS)

F32 = mybir.dt.float32
BF16 = mybir.dt.bfloat16
I32 = mybir.dt.int32
U32 = mybir.dt.uint32
U16 = mybir.dt.uint16
U8 = mybir.dt.uint8
FP8X4 = mybir.dt.float8_e4m3fn_x4
FP4X4 = mybir.dt.float4_e2m1fn_x4
ACT = mybir.ActivationFunctionType
ALU = mybir.AluOpType

P = 128
PACK = 4
PASS = P * PACK
K_PASSES = K // PASS
H_PASSES = H // PASS
QUADRANTS = 4
BLOCK_ROWS = 8
BANK = 512
QUARTER = BANK // PACK
HALF = PAIRS // 2
LIST_ROWS = 16


def tile_list_bidding_tutor_reading_kernel(
    tc, tab_words, tab_scales, offs, pos1, pos2, w1, w2_words, w2_scales, w3,
    w4_words, w4_scales, temp, shift, steep, share, gain, stance, lift, out,
):
    nc = tc.nc
    with ExitStack() as ctx:
        keep = ctx.enter_context(tc.tile_pool(name="keep", bufs=1))
        psum = ctx.enter_context(tc.psum_pool(name="psum", bufs=1))

        def kept(shape, dtype, name, tag=None):
            return keep.tile(shape, dtype, name=name, tag=tag or name, align_bytes=64)

        def bank_tile(bank, name):
            return psum.tile([P, BANK], F32, name=name, tag="bank%d" % bank)

        def load_list(src, name):
            tile = keep.tile(list(src.shape), U16, name=name)
            nc.sync.dma_start(tile[:], src)
            return tile

        def load_row_factor(src, name):
            tile = kept([P, H_PASSES, PACK], F32, name)
            nc.sync.dma_start(out=tile[:], in_=src.rearrange("(b p i) -> p b i", p=P, i=PACK))
            return tile

        def load_w1(a, b, tag):
            raw = kept([P, PACK, PASS], F32, "w1_raw%d%d" % (a, b), tag)
            piece = w1[a * PASS:(a + 1) * PASS, b * PASS:(b + 1) * PASS]
            nc.sync.dma_start(out=raw[:], in_=piece.rearrange("(p j) c -> p j c", j=PACK))
            return raw

        def load_table(a):
            tile = kept([P, T], U32, "tab%d" % a)
            nc.sync.dma_start(out=tile[:].bitcast(I32), in_=tab_words[a].rearrange("p t i -> p (t i)").bitcast(I32))
            return tile

        def load_plane(plane, src):
            for q in range(QUADRANTS):
                nc.sync.dma_start(
                    out=plane[32 * q:32 * q + 4, :, :].bitcast(I32),
                    in_=src[:, 4 * q:4 * q + 4, :].rearrange("a r n -> r a n").bitcast(I32),
                )

        tab_plane = kept([P, T], U8, "tab_plane")
        w2_plane_raw = kept([P, H_PASSES, R], U8, "w2_plane_raw")
        w4_plane = kept([P, H_PASSES, N], U8, "w4_plane")
        for plane in (tab_plane, w2_plane_raw, w4_plane):
            nc.vector.memset(plane[:].bitcast(I32), 0)
        for q in range(QUADRANTS):
            nc.gpsimd.dma_start(
                out=tab_plane[32 * q:32 * q + 4 * K_PASSES, :].bitcast(I32),
                in_=tab_scales[:, 4 * q:4 * q + 4, :].bitcast(I32),
            )

        w1_raw = {}
        tab = {}
        w1_raw[0, 0] = load_w1(0, 0, "stage_a")
        offs_t = load_list(offs, "offs_t")
        tab[0] = load_table(0)
        w1_raw[1, 0] = load_w1(1, 0, "stage_b")
        tab[1] = load_table(1)
        tab[2] = load_table(2)
        w1_raw[2, 0] = load_w1(2, 0, "stage_c")
        pos1_t = load_list(pos1, "pos1_t")
        temp_t = load_row_factor(temp, "temp_t")
        shift_t = load_row_factor(shift, "shift_t")
        w1_raw[0, 1] = load_w1(0, 1, "stage_d")
        w1_raw[1, 1] = load_w1(1, 1, "stage_a")
        pos2_t = load_list(pos2, "pos2_t")
        steep_t = load_row_factor(steep, "steep_t")
        share_t = load_row_factor(share, "share_t")
        w2_raw = kept([P, H_PASSES, 2 * R], U8, "w2_raw")
        nc.sync.dma_start(out=w2_raw[:].bitcast(I32), in_=w2_words.rearrange("a p n -> p a n").bitcast(I32))
        w1_raw[2, 1] = load_w1(2, 1, "stage_b")
        load_plane(w2_plane_raw, w2_scales)
        gain_t = load_row_factor(gain, "gain_t")
        stance_t = load_row_factor(stance, "stance_t")
        w4_codes = kept([P, H_PASSES, N], U32, "w4_codes")
        nc.sync.dma_start(out=w4_codes[:].bitcast(I32), in_=w4_words.rearrange("a p c i -> p a (c i)").bitcast(I32))
        w3_raw = kept([P, PACK, N], F32, "w3_raw", "stage_c")
        for t in range(PACK):
            nc.sync.dma_start(
                out=w3_raw[:, t, :], in_=w3.rearrange("(g t u) n -> t g u n", t=PACK, u=BLOCK_ROWS)[t])
        lift_raw = kept([P, PACK, 8], F32, "lift_raw")
        lift_t = kept([P, 1, PACK], F32, "lift_t")
        with nc.allow_non_contiguous_dma(reason="one factor a partition"):
            for t in range(PACK):
                nc.sync.dma_start(
                    out=lift_raw[:, t, 0:1],
                    in_=lift.rearrange("(g t u o) -> t g u o", t=PACK, u=BLOCK_ROWS, o=1)[t])
        nc.gpsimd.tensor_copy(out=lift_t[:, 0, :], in_=lift_raw[:, :, 0])
        load_plane(w4_plane, w4_scales)

        def quantise(codes, plane, rounded):
            nc.vector.quantize_mx(out=codes.bitcast(FP8X4), scales=plane, in_=rounded.rearrange("p c i -> p (c i)"))

        picked = {}
        picked_plane = kept([P, S], U8, "picked_plane")
        w1_codes = {}
        w1_plane = {}
        for a in range(K_PASSES):
            for b in range(H_PASSES):
                w1_codes[a, b] = kept([P, PASS], U32, "w1_codes%d%d" % (a, b))
                w1_plane[a, b] = kept([P, PASS], U8, "w1_plane%d%d" % (a, b))

        def gather_words(a):
            picked[a] = kept([P, S], U32, "picked%d" % a)
            nc.vector.tensor_copy(out=picked[a][:], in_=tab[a][:].indirect(offs_t[:]))

        def round_w1(engine, a, b, tiles, tag):
            rounded = kept([P, len(tiles), P, PACK], BF16, "w1_bf16", tag)
            src = w1_raw[a, b][:].rearrange("p j (m i) -> p m i j", i=PACK)[:, :, tiles.start:tiles.stop, :]
            dst = rounded[:].rearrange("p i m j -> p m i j")
            if engine == "scalar":
                nc.scalar.activation(
                    out=dst.rearrange("p m i j -> p m j i"), in_=src.rearrange("p m i j -> p m j i"), func=ACT.Copy)
            elif engine == "gpsimd":
                for m0 in (0, P // 2):
                    nc.gpsimd.tensor_scalar(
                        out=dst[:, m0:m0 + P // 2, :, :], in0=src[:, m0:m0 + P // 2, :, :],
                        scalar1=1.0, scalar2=0.0, op0=ALU.mult, op1=ALU.add)
            else:
                nc.vector.tensor_copy(out=dst, in_=src)
            return {i: (rounded, i - tiles.start) for i in tiles}

        def quantise_w1(a, b, rounded, tiles):
            tile, place = rounded[tiles.start]
            cols = slice(tiles.start * P, tiles.stop * P)
            quantise(w1_codes[a, b][:, cols], w1_plane[a, b][:, cols],
                     tile[:, place:place + len(tiles), :, :].rearrange("p i m j -> p (i m) j"))

        every, front, back = range(PACK), range(PACK // 2), range(PACK // 2, PACK)
        gather_words(0)
        nc.vector.tensor_copy(out=picked_plane[:], in_=tab_plane[:].indirect(offs_t[:]))
        quantise_w1(0, 0, round_w1("scalar", 0, 0, every, "round_a"), every)
        quantise_w1(1, 0, round_w1("scalar", 1, 0, every, "round_b"), every)
        gather_words(1)
        gather_words(2)
        last_front = round_w1("vector", 2, 0, front, "round_c")
        last_back = round_w1("scalar", 2, 0, back, "round_d")
        for i in front:
            quantise_w1(2, 0, last_front, range(i, i + 1))
        quantise_w1(2, 0, last_back, back)

        h = {}
        h_acc = {}
        bank_top = kept([P, H_PASSES, PACK, S // BANK], F32, "bank_top")
        gate_bias = kept([P, H_PASSES, PACK], F32, "gate_bias")
        gate_slope = kept([P, H_PASSES, PACK], F32, "gate_slope")
        gate_gain = kept([P, H_PASSES, PACK], F32, "gate_gain")

        def score_pass(b, i, u, a):
            cols = slice(i * P, (i + 1) * P)
            hands = slice(u * BANK, (u + 1) * BANK)
            nc.tensor.matmul_mx(
                out=h_acc[b, i, u][:],
                lhsT=w1_codes[a, b][:, cols].bitcast(FP8X4),
                lhsT_scale=w1_plane[a, b][:, cols],
                rhs=picked[a][:, hands].bitcast(FP8X4),
                rhs_scale=picked_plane[4 * a:P, hands],
                start=(a == 0),
                stop=(a == K_PASSES - 1),
            )

        def early_passes(b):
            for i in every:
                for u in range(S // BANK):
                    h_acc[b, i, u] = bank_tile(2 * i + u, "h_acc")
            for a in range(K_PASSES - 1):
                for i in every:
                    for u in range(S // BANK):
                        score_pass(b, i, u, a)

        scalar_bank = (0, 0, 1)

        def finish_scores(b, i):
            h[b, i] = kept([P, S], F32, "h%d%d" % (b, i))
            for u in range(S // BANK):
                score_pass(b, i, u, K_PASSES - 1)
                dst = h[b, i][:, u * BANK:(u + 1) * BANK]
                if (b, i, u) == scalar_bank:
                    nc.scalar.copy(out=dst, in_=h_acc[b, i, u][:])
                else:
                    nc.vector.tensor_scalar(
                        out=dst, in0=h_acc[b, i, u][:], scalar1=1.0, scalar2=None,
                        op0=ALU.mult, op1=ALU.max, accum_out=bank_top[:, b, i, u:u + 1])

        def look_exp(dst, b, i, places):
            nc.scalar.activation(
                out=dst[:, places],
                in_=h[b, i][:].indirect(pos1_t[:, places.start // LIST_ROWS:places.stop // LIST_ROWS]),
                func=ACT.Exp, scale=temp_t[:, b, i:i + 1], bias=shift_t[:, b, i:i + 1],
            )

        def look_sigmoid(dst, b, i):
            nc.scalar.activation(
                out=dst[:], in_=h[b, i][:].indirect(pos2_t[:]),
                func=ACT.Sigmoid, scale=steep_t[:, b, i:i + 1], bias=gate_bias[:, b, i:i + 1],
            )

        all_places = slice(0, PAIRS)
        open0 = [kept([P, PAIRS], F32, "open0_%d" % i) for i in every]
        early_passes(0)
        next_front = round_w1("gpsimd", 0, 1, front, "round_c")
        for i in every:
            if i == PACK - 1:
                quantise_w1(0, 1, next_front, front)
            finish_scores(0, i)
            look_exp(open0[i], 0, i, all_places)

        minus_share = kept([P, H_PASSES, PACK], F32, "minus_share")
        nc.gpsimd.tensor_scalar(
            out=minus_share[:], in0=share_t[:], scalar1=-1.0, scalar2=0.0, op0=ALU.mult, op1=ALU.add)
        nc.gpsimd.tensor_tensor(out=gate_slope[:], in0=steep_t[:], in1=minus_share[:], op=ALU.mult)
        top0 = kept([P, PACK], F32, "top0")
        nc.vector.tensor_reduce(
            out=bank_top[:, 0, 0, 1:2], in_=h[0, 0][:, BANK:S], axis=mybir.AxisListType.X, op=ALU.max)
        nc.vector.tensor_tensor(out=top0[:], in0=bank_top[:, 0, :, 0], in1=bank_top[:, 0, :, 1], op=ALU.max)
        nc.vector.tensor_tensor(out=gate_bias[:, 0, :], in0=top0[:], in1=gate_slope[:, 0, :], op=ALU.mult)
        gate0 = [kept([P, PAIRS], F32, "gate0_%d" % i) for i in every]
        for i in every:
            look_sigmoid(gate0[i], 0, i)

        quantise_w1(0, 1, round_w1("vector", 0, 1, back, "round_d"), back)
        quantise_w1(1, 1, round_w1("vector", 1, 1, every, "round_a"), every)
        last_piece = round_w1("vector", 2, 1, every, "round_b")
        quantise_w1(2, 1, last_piece, front)
        quantise_w1(2, 1, last_piece, back)
        early_passes(1)

        def second_half_looks(name):
            first = kept([P, PACK - 1, PAIRS], F32, name + "_first", "looks1_first")
            last = kept([P, PAIRS], F32, name + "_last", "looks1_last")
            return [first[:, i, :] for i in range(PACK - 1)] + [last[:]]

        gate1 = second_half_looks("gate1")
        for i in every:
            finish_scores(1, i)
            nc.vector.tensor_scalar(
                out=gate_bias[:, 1, i:i + 1], in0=bank_top[:, 1, i, 0:1], scalar1=bank_top[:, 1, i, 1:2],
                scalar2=gate_slope[:, 1, i:i + 1], op0=ALU.max, op1=ALU.mult)
            look_sigmoid(gate1[i], 1, i)

        nc.gpsimd.tensor_tensor(out=gate_gain[:], in0=gain_t[:], in1=stance_t[:], op=ALU.mult)
        open0_scaled = kept([P, PACK, PAIRS], F32, "open0_scaled", "stage_b")
        for i in every:
            nc.gpsimd.tensor_scalar(
                out=open0_scaled[:, i, :], in0=open0[i][:], scalar1=stance_t[:, 0, i:i + 1], scalar2=0.0,
                op0=ALU.mult, op1=ALU.add)
        gate1_scaled = kept([P, PACK, PAIRS], F32, "gate1_scaled")
        for i in every:
            nc.vector.tensor_scalar(
                out=gate1_scaled[:, i, :], in0=gate1[i], scalar1=gate_gain[:, 1, i:i + 1], scalar2=None,
                op0=ALU.mult)
        open1 = second_half_looks("open1")
        halves = [slice(u * HALF, (u + 1) * HALF) for u in range(PAIRS // HALF)]
        for places in halves:
            for i in every:
                look_exp(open1[i], 1, i, places)

        pair_rows = [kept([P, PACK, PAIRS], BF16, "pair_rows%d" % b) for b in range(H_PASSES)]
        pair_bf16 = [kept([P, PAIRS, PACK], BF16, "pair_bf16%d" % b) for b in range(H_PASSES)]
        pair_codes = [kept([P, PAIRS], U32, "pair_codes%d" % b) for b in range(H_PASSES)]
        pair_plane = [kept([P, PAIRS], U8, "pair_plane%d" % b) for b in range(H_PASSES)]

        def join(b, later, factor, earlier_scaled, places):
            for i in every:
                nc.vector.scalar_tensor_tensor(
                    out=pair_rows[b][:, i, places], in0=later[i][:, places], scalar=factor[:, b, i:i + 1],
                    in1=earlier_scaled[:, i, places], op0=ALU.mult, op1=ALU.add)

        def interleave_pair(b, places):
            nc.vector.tensor_copy(
                out=pair_bf16[b][:, places, :].rearrange("p (c x) i -> p c i x", x=4),
                in_=pair_rows[b][:, :, places].rearrange("p i (c x) -> p c i x", x=4),
            )

        def quantise_pair(b, places):
            quantise(pair_codes[b][:, places], pair_plane[b][:, places], pair_bf16[b][:, places, :])

        join(0, gate0, gate_gain, open0_scaled, all_places)
        interleave_pair(0, all_places)
        quantise_pair(0, all_places)

        w2_codes = kept([P, H_PASSES, 2 * R], U8, "w2_codes")
        w2_plane = kept([P, H_PASSES, R], U8, "w2_plane")
        for dst, src in ((w2_codes, w2_raw), (w2_plane, w2_plane_raw)):
            nc.gpsimd.tensor_copy(
                out=dst[:].bitcast(I32).rearrange("p a (t g w) -> p a t g w", t=PACK, g=P // BLOCK_ROWS),
                in_=src[:].bitcast(I32).rearrange("p a (g t w) -> p a t g w", t=PACK, g=P // BLOCK_ROWS),
            )
        w3_bf16 = kept([P, N, PACK], BF16, "w3_bf16", "round_b")
        w3_codes = kept([P, N], U32, "w3_codes")
        w3_plane = kept([P, N], U8, "w3_plane")
        for c0 in (0, N // 2):
            nc.gpsimd.tensor_scalar(
                out=w3_bf16[:, c0:c0 + N // 2, :], in0=w3_raw[:, :, c0:c0 + N // 2].rearrange("p t c -> p c t"),
                scalar1=1.0, scalar2=0.0, op0=ALU.mult, op1=ALU.add)
        quantise(w3_codes[:], w3_plane[:], w3_bf16[:])

        quarters = [slice(q * QUARTER, (q + 1) * QUARTER) for q in range(PAIRS // QUARTER)]
        pupil_acc = [bank_tile(q, "pupil_acc") for q in range(len(quarters))]
        out_acc = [bank_tile(len(quarters) + q, "out_acc") for q in range(len(quarters))]

        def pupil_passes(q, b):
            for t in range(PACK):
                nc.tensor.matmul_mx(
                    out=pupil_acc[q][:, t * QUARTER:(t + 1) * QUARTER],
                    lhsT=w2_codes[:, b, 2 * t * P:2 * (t + 1) * P].bitcast(FP4X4),
                    lhsT_scale=w2_plane[:, b, t * P:(t + 1) * P],
                    rhs=pair_codes[b][:, quarters[q]].bitcast(FP8X4),
                    rhs_scale=pair_plane[b][:, quarters[q]],
                    start=(b == 0 and t == 0),
                    stop=(b == H_PASSES - 1 and t == PACK - 1),
                )

        def out_passes(q, w_codes, w_plane, x_codes, x_plane, first, last):
            for s in range(N // P):
                nc.tensor.matmul_mx(
                    out=out_acc[q][:, s * QUARTER:(s + 1) * QUARTER],
                    lhsT=w_codes[:, s * P:(s + 1) * P].bitcast(FP8X4),
                    lhsT_scale=w_plane[:, s * P:(s + 1) * P],
                    rhs=x_codes[:, quarters[q]].bitcast(FP8X4),
                    rhs_scale=x_plane[:, quarters[q]],
                    start=(first and s == 0),
                    stop=(last and s == N // P - 1),
                )

        bent = kept([P, PAIRS, PACK], F32, "bent", "stage_a")
        result = kept([P, len(quarters), N // P, QUARTER], F32, "result", "stage_d")
        pupil_bf16 = kept([P, PAIRS, PACK], BF16, "pupil_bf16")
        pupil_codes = kept([P, PAIRS], U32, "pupil_codes")
        pupil_plane = kept([P, PAIRS], U8, "pupil_plane")
        out_rows = out.rearrange("(s p) j -> p s j", p=P)

        def bend(q):
            nc.scalar.activation(
                out=bent[:, quarters[q], :], in_=pupil_acc[q][:].rearrange("p (t j) -> p j t", t=PACK), func=ACT.Tanh)

        def round_pupil(places):
            nc.vector.tensor_tensor(
                out=pupil_bf16[:, places, :], in0=bent[:, places, :],
                in1=lift_t[:].to_broadcast([P, places.stop - places.start, PACK]), op=ALU.mult)

        def quantise_pupil(places):
            quantise(pupil_codes[:, places], pupil_plane[:, places], pupil_bf16[:, places, :])

        def finish_out(q, copy):
            out_passes(q, w3_codes[:], w3_plane[:], pupil_codes, pupil_plane, False, True)
            copy(out=result[:, q, :, :].rearrange("p s j -> p (s j)"), in_=out_acc[q][:])
            nc.sync.dma_start(out=out_rows[:, :, quarters[q]], in_=result[:, q, :, :])

        for q in range(len(quarters)):
            pupil_passes(q, 0)
        for u, places in enumerate(halves):
            join(1, open1, stance_t, gate1_scaled, places)
            for q in (2 * u, 2 * u + 1):
                interleave_pair(1, quarters[q])
            for q in (2 * u, 2 * u + 1):
                quantise_pair(1, quarters[q])
                pupil_passes(q, 1)
                bend(q)
        for q in range(len(quarters)):
            for b in range(H_PASSES):
                out_passes(q, w4_codes[:, b, :], w4_plane[:, b, :], pair_codes[b], pair_plane[b], b == 0, False)
        round_pupil(halves[0])
        quantise_pupil(halves[0])
        finish_out(0, nc.scalar.copy)
        finish_out(1, nc.scalar.copy)
        round_pupil(quarters[2])
        round_pupil(quarters[3])
        for q, copy in ((2, nc.scalar.copy), (3, nc.vector.tensor_copy)):
            quantise_pupil(quarters[q])
            finish_out(q, copy)
